import numpy as np, ml_dtypes
CORES = [35,38,43,46]
N = 4
BF = ml_dtypes.bfloat16
def gentries(a):
    return np.ascontiguousarray(a.reshape(8, 16, -1).transpose(0, 2, 1)).reshape(8, -1)
def gtable(e):
    e = np.asarray(e); return np.ascontiguousarray(e.reshape(8, -1, 16).transpose(0, 2, 1)).reshape(128, -1).astype(np.int32)
W, K, RO, S, TH, AG = 3072, 256, 3, 4, 68, 9
L0 = 16 - RO
B = K // N
def hubbed(rng, hub, n, share):
    return np.where(rng.random((N, 8, n)) < share, np.take_along_axis(hub, rng.integers(0, 32, (N, 8, n)), 2), rng.integers(0, W, (N, 8, n)))
def parts(rng):
    x = np.where(rng.random((N, 8, 1, W)) < 0.875, rng.integers(0, 16, (N, 8, 16, W)), rng.integers(4, 12, (N, 8, 16, W)))
    hub = rng.integers(0, W, (N, 8, 32)); a = hubbed(rng, hub, L0 * W, 0.1).reshape(N, 8, L0, W)
    a = np.where(rng.random(a.shape) < rng.choice(np.array([0.05, 0.2, 0.45]), (N, 8, 1, 1)), -1, a)
    return x, a, hubbed(rng, hub, W, 0.25), rng.integers(0, W, (N, 8, K))
def pack(x, a, s, p):
    a = np.concatenate([a, np.full((N, 8, RO, W), -1)], axis=2)
    return {"x0": np.ascontiguousarray(x.reshape(N, 128, W)).astype(np.float32).astype(BF), "lk": np.ascontiguousarray(a.reshape(N, 128, W)).astype(np.int32),
            "nx": np.ascontiguousarray(s).astype(np.int32), "w0": np.stack([gtable(e) for e in p])}
def setup_inputs(rng):
    return pack(*parts(rng))
def setup_inputs_ties(rng):
    x, a, s, p = parts(rng); h = W // 2
    x[..., :h] = rng.integers(0, 16, (N, 8, 16, h))
    t = TH - 1 + rng.integers(0, 3, (N, 8, 1, h)); o = np.argsort(rng.random((N, 8, 16, h)), axis=2)
    x[..., h:2 * h] = x[..., :h] + np.where(x[..., :h] < 8, 1, -1) * ((t >> 4) + (o < (t & 15)))
    i = np.arange(L0)[None, None, :, None]; at = rng.integers(0, L0, (N, 8, 1, h)); bare = rng.random((N, 8, 1, h)) < 0.5
    a[..., :h] = np.where(i == at, h + np.arange(h), np.where((i > at) | bare, -1, a[..., :h]))
    return pack(x, a, s, rng.integers(0, h, (N, 8, K)))
def setup_inputs_votes(rng):
    x, a, s, p = parts(rng); h = K // 2
    for q in range(N):
        for g in range(8):
            if q < N - 1 and g % 4 == 3: continue
            c = rng.permutation(W)[:K * (S + 1)].reshape(K, S + 1); a[q, g] = -1
            s[q, g, c[:, :S]] = c[:, 1:]
            if q == N - 1:
                y = rng.integers(5, 8, (16, K, S)); e = np.where(np.arange(K) < h, 15, rng.integers(8, 11, (16, K)))
                s[q, g, c[:h, S]] = c[h + rng.permutation(h), 2]
                p[q, g] = c[:, 0]
            elif g % 2 == 1:
                n = K - 1 if g == 1 else int(rng.integers(h, K))
                y = rng.integers(0, 8, (16, K, S)); y[rng.permutation(16)[AG - 1:], n] += 8
                e = rng.integers(0, 16, (16, K)); e[:, 0] = 8
                s[q, g, c[:, S - 1]] = c[0, S]
                p[q, g] = c[:, 0]
            else:
                y = rng.integers(2, 14, (16, K, S)); y[:, h:] = np.where(rng.random((1, K - h, 1)) < 0.5, 2, 13)
                z = y[:, :, 0]
                for k in range(1, S): z = (z + y[:, :, k]) >> 1
                o = np.argsort(rng.random((16, K)), axis=0); n = AG - 1 + rng.integers(0, 3, (1, K))
                e = z + np.where(o < n, rng.integers(1, 3, (16, K)), -rng.integers(0, 2, (16, K)))
                s[q, g, c[h:, S - 1]] = np.where(rng.random(K - h) < 0.75, c[:K - h, S], c[h:, S])
                p[q, g] = c[rng.permutation(K), 0]
            x[q, g][:, c[:, :S].reshape(-1)] = y.reshape(16, K * S); x[q, g][:, c[:, S]] = e
    return pack(x, a, s, p)
def setup_inputs_alike(rng):
    x, a, s, p = parts(rng); few = np.array([0, W - 1, W // 2, 5])
    a[:, ::2] = np.where(a[:, ::2] < 0, -1, rng.choice(few, (N, 4, L0, W)))
    a[:, 1] = np.where(a[:, 1] < 0, -1, np.arange(W)); s[:, 1] = np.arange(W)
    s[:, 0] = W - 1; s[:, 4] = 0; s[:, 2] = rng.choice(few, (N, W))
    p[:, 3] = p[:, 3, :1]; p[:, 5] = rng.choice(few, (N, K)); p[:, 6] = np.where(rng.random((N, K)) < 0.5, 0, W - 1)
    return pack(x, a, s, p)
def setup_inputs_full(rng):
    x, a, s, p = parts(rng)
    x[:, ::2] = rng.integers(6, 10, (N, 4, 16, W)); x[:, 1::2] = 15 * rng.integers(0, 2, (N, 4, 16, W))
    a = np.where(a < 0, rng.integers(0, W, a.shape), a)
    return pack(x, a, s, p)
def setup_inputs_spread(rng):
    x, a, s, p = parts(rng)
    x = np.minimum((np.exp2(1 + 3 * rng.random((N, 8, 1, W))) * rng.random((N, 8, 16, W))).astype(np.int64), 15)
    a = np.where(a < 0, -1, (W * rng.random(a.shape) ** 3).astype(np.int64)); s = (W * rng.random(s.shape) ** 2).astype(np.int64)
    return pack(x, np.minimum(a, W - 1), np.minimum(s, W - 1), p)
def check_inputs(d):
    bad = []
    x = d["x0"].astype(np.float32)
    if not np.all((x >= 0) & (x <= 15) & (x == np.floor(x))): bad.append("x0 whole numbers from 0 to 15")
    for k, lo in (("lk", -1), ("nx", 0), ("w0", 0)):
        if np.min(d[k]) < lo or np.max(d[k]) > W - 1: bad.append("range of " + k)
    if np.any(d["lk"].reshape(-1, 8, 16, W)[:, :, L0:] != -1): bad.append("upper links of lk empty")
    return bad
def reference(x0, lk, nx, w0):
    M = W + RO * K
    X = np.zeros((N, 8, 16, M), np.int64); X[..., :W] = x0.astype(np.float32).astype(np.int64).reshape(N, 8, 16, W)
    ad = np.full((N, 8, 16, M), -1, np.int64); ad[..., :W] = lk.reshape(N, 8, 16, W)
    sc = np.zeros((N, 8, M), np.int64); sc[..., :W] = nx
    v = np.stack([gentries(e) for e in w0]).astype(np.int64)
    i = np.arange(16)[:, None]
    for t in range(RO):
        n = W + t * K; Z = np.zeros((N, 8, 16, K), np.int64)
        for r in range(N):
            for g in range(8):
                x, a, s, p = X[r, g], ad[r, g], sc[r, g], v[r, g]
                z = x[:, p]; l = np.full(K, 16)
                for k in range(S):
                    c = a[:, p]
                    dist = np.add.reduce(np.abs(x[:, np.maximum(c, 0)] - z[:, None, :]), axis=0)
                    b = np.max(np.where((c >= 0) & (dist < TH) & (i < l), i, -1), axis=0)
                    p = np.where(b >= 0, c[np.maximum(b, 0), np.arange(K)], s[p]); l = np.where(b >= 0, b, l)
                    y = x[:, p]; yes = np.add.reduce((y > z).astype(np.int64), axis=0) >= AG
                    z = (z + y) >> 1
                Z[r, g] = z; v[r, g] = p
                ends = np.zeros(M, bool); ends[p] = True
                no = np.zeros(M, bool); no[p[~yes]] = True
                x[::2] = np.where(ends & ~no, 15 - x[::2], x[::2])
                u, first = np.unique(p, return_index=True)
                a[L0 + t, u] = n + first; s[n:n + K] = s[p]
        for r in range(N):
            for q in range(N):
                X[q, :, :, n + r * B:n + (r + 1) * B] = np.roll(Z[r, :, :, q * B:(q + 1) * B], (q - r) % N, axis=0)
    return {"yx": X.reshape(N, 128, M).astype(np.float32).astype(BF), "yv": v.astype(np.float32)}

@@ -1,0 +1,519 @@
+import numpy as np
+from concourse.bass import DstId, RemoteDMATransfer
+from concourse.mybir import AluOpType, ActivationFunctionType
+
+ALU = AluOpType
+ACT = ActivationFunctionType
+
+W0N, K, RO, S = 3072, 256, 3, 4
+B = 272
+CEN = 1919
+XC = B + W0N + RO * K
+AC = B + W0N + (RO - 1) * K
+CYC = 0.00083
+PEC = 0.00055
+GAT = 1.45
+WK = 0.08
+
+SCRATCH = {}
+
+
+def _b(name, cols, dtype, where="sbuf"):
+    SCRATCH[name] = (where, [128, cols], dtype)
+
+
+_b("X", XC, "bfloat16")
+_b("A", AC, "int32")
+_b("WL", 16, "int32")
+for _n in ("NL", "OFF", "OFX"):
+    _b(_n, 16, "uint16")
+for _u in "01":
+    for _n in ("z", "ok", "s", "gt"):
+        _b(_n + _u, 128, "bfloat16")
+    for _n in ("AT", "T1", "sA"):
+        _b(_n + _u, 128, "float16")
+    for _n in ("sc", "sv", "s2"):
+        _b(_n + _u, 128, "float32")
+    _b("LT" + _u, 128, "uint16")
+    _b("xg" + _u, 1920, "bfloat16")
+    _b("mn" + _u, 1920, "bfloat16")
+    for _s in "0123":
+        _b("sel" + _s + _u, 128, "bfloat16")
+    for _n in ("pz", "pd", "pc", "pe"):
+        _b(_n + _u, 512, "float32", "psum")
+_b("yg", 256, "bfloat16")
+_b("vb", 256, "float16")
+for _n in ("vT", "vX", "wt", "ofs", "fe", "ff", "fm", "fo", "TR"):
+    _b(_n, 16, "float32")
+_b("EQ", 16 * 256, "bfloat16")
+for _n in ("scL", "AF", "VA", "vout", "J", "JM", "ta", "tb", "tc", "td", "RS", "NW0", "NW1"):
+    _b(_n, 256, "float32")
+_b("VX", 256, "bfloat16")
+_b("snd", 192, "bfloat16")
+_b("PI", 4, "int32")
+_b("col", 32, "float32")
+_b("JG", 128, "float32")
+_b("JP", 128, "float32")
+_b("W1", 144, "bfloat16")
+_b("W2", 144, "bfloat16")
+for _n in ("BOb", "NBb", "FBb", "MTb", "ZS", "DEAD", "TRI0", "TRI1", "TRI2", "IDb", "PM1", "PM2", "PM3"):
+    _b(_n, 128, "bfloat16")
+for _n in ("BOh", "IDh", "SW00", "SW01", "SW10", "SW11", "MK0"):
+    _b(_n, 128, "float16")
+_b("MKl", 256, "float16")
+_b("MK2", 256, "float16")
+
+SEMAPHORES = ["qV", "qS", "qP", "qG", "dX", "dW", "dA", "dO", "arr0", "arr1", "arr2", "snt"]
+
+
+def rank_program(g, core, T, topo):
+    rank = T.rank_of(core)
+    if rank is None:
+        return
+    QUE = {"V": g.vector, "S": g.scalar, "P": g.tensor, "G": g, "Y": g.sync}
+    recs = []
+    stage = [0]
+
+    def rec(q, kind, fn, reads, writes, dur, lat=0.0, sem=None):
+        recs.append((q, kind, fn, tuple(reads), tuple(writes), dur, lat, sem, stage[0]))
+
+    def op(q, fn, reads, writes, dur):
+        rec(q, "op", fn, reads, writes, dur)
+
+    def dma(q, out, in_, sem, reads, writes, lat):
+        rec(q, "dma", lambda: QUE[q].dma_start(out, in_), reads, writes, 0.06, lat, sem)
+
+    def vd(n, f=1.0, ind=None):
+        return max(64, n * f) * CYC if ind is None else 0.05 + n * CYC * ind
+
+    def ts(out, in0, s1, s2, op0, op1, reads, writes, n=128, f=1.0, ind=None):
+        if op1 is None:
+            op("V", lambda: g.vector.tensor_scalar(out, in0, s1, s2, op0), reads, writes, vd(n, f, ind))
+        else:
+            op("V", lambda: g.vector.tensor_scalar(out, in0, s1, s2, op0, op1), reads, writes, vd(n, f, ind))
+
+    def tt(out, in0, in1, o, reads, writes, n=128, f=1.0, ind=None):
+        op("V", lambda: g.vector.tensor_tensor(out, in0, in1, o), reads, writes, vd(n, f, ind))
+
+    def cp(out, in_, reads, writes, n, ind=None):
+        op("V", lambda: g.vector.tensor_copy(out, in_), reads, writes, vd(n, 1.0, ind))
+
+    def act(out, in_, f, bias, scale, reads, writes, n=128, ind=1.0):
+        op("S", lambda: g.scalar.activation(out, in_, f, bias=bias, scale=scale), reads, writes, 0.065 + n * CYC * ind)
+
+    def scn(out, data1, n, reads, writes):
+        op("V", lambda: g.vector.tensor_tensor_scan(out, T.RS[:, 0:n], data1, 0.0, ALU.mult, ALU.max), ["RS"] + reads, writes, vd(n))
+
+    def mms(lst, reads, writes, n=128):
+        def go():
+            r = None
+            for (o, l, r_, st, sp) in lst:
+                r = g.tensor.matmul(o, l, r_, st, sp)
+            return r
+        op("P", go, reads, writes, len(lst) * n * PEC)
+
+    dma("Y", T.WL[:], T.w0[:], "dW", [], ["WL"], 2.0)
+    dma("Y", T.X[:, B:B + W0N], T.x0[:], "dX", [], ["X"], 5.0)
+    for gr in range(8):
+        dma("S" if gr % 2 == 0 else "Y", T.A[16 * gr:16 * gr + 15, B:B + W0N], T.lk[16 * gr:16 * gr + 15, :], "dA", [], ["A%d" % gr], 9.0)
+    dma("S", T.A[15:128:16, B:B + W0N], T.nx[:], "dA", [], ["A8"], 9.0)
+    AK = ["A%d" % i for i in range(9)] + ["Am"]
+    XK = ["X", "Xm"]
+
+    CI = {}
+
+    def newcol(name):
+        CI[name] = len(CI)
+        return col(name)
+
+    def col(name):
+        i = CI[name]
+        return T.col[:, i:i + 1]
+
+    def iota(ap, key, pattern, base, cm, n, whole=False):
+        if whole:
+            op("G", lambda: g.iota(ap, pattern, base, cm), [], [key], 0.13 + 2 * CYC * n)
+        else:
+            op("G", lambda: g.iota(ap, pattern, base, cm, allow_small_or_imprecise_dtypes=True), [], [key], 0.13 + 2 * CYC * n)
+
+    iota(T.PI[:, 0:1], "PI", [[0, 1]], 0, 1, 1, True)
+    iota(T.JG[:], "JG", [[16, 8], [0, 16]], 0, 0, 128)
+    iota(T.J[:], "J", [[1, 256]], 0, 0, 256)
+    iota(T.JM[:], "JM", [[0, 16], [1, 16]], 0, 0, 256)
+
+    def mkcol(name, in0, s1, s2, op0, op1, reads):
+        ts(newcol(name), in0, s1, s2, op0, op1, reads, ["c" + name], 1)
+
+    ts(T.NL[:], T.WL[:], float(B), None, ALU.add, None, ["WL"], ["NL0", "NL1"], 16)
+    op("V", lambda: g.vector.memset(T.A[:, 0:B], -1), [], ["Am"], vd(B))
+    op("V", lambda: g.vector.memset(T.X[:, 0:B], 95.0), [], ["Xm"], vd(B, 0.5))
+    ts(T.PI[:, 1:2], T.PI[:, 0:1], 15, None, ALU.bitwise_and, None, ["PI"], ["PI1"], 1)
+    ts(T.PI[:, 2:3], T.PI[:, 0:1], 16, None, ALU.bitwise_and, None, ["PI"], ["PI2"], 1)
+    ts(T.PI[:, 3:4], T.PI[:, 0:1], 1, None, ALU.bitwise_and, None, ["PI"], ["PI3"], 1)
+    for n_, a in (("P", 0), ("Pm16", -16), ("Pp16", 16), ("Pp32", 32), ("Pp48", 48), ("Pm112", -112), ("Pm96", -96), ("Pm80", -80)):
+        mkcol(n_, T.PI[:, 0:1], float(a), None, ALU.add, None, ["PI"])
+    mkcol("R", T.PI[:, 1:2], 0.0, None, ALU.add, None, ["PI1"])
+    mkcol("U1", T.PI[:, 2:3], 0.0625, None, ALU.mult, None, ["PI2"])
+    mkcol("U0", T.PI[:, 2:3], -0.0625, 1.0, ALU.mult, ALU.add, ["PI2"])
+    mkcol("fs", T.PI[:, 3:4], 2.0, -1.0, ALU.mult, ALU.add, ["PI3"])
+    mkcol("fb", T.PI[:, 3:4], -335.0, 175.0, ALU.mult, ALU.add, ["PI3"])
+    tt(newcol("G"), col("P"), col("R"), ALU.subtract, ["cP", "cR"], ["cG"], 1)
+    mkcol("G15", col("G"), 15.0, None, ALU.add, None, ["cG"])
+    mkcol("m15", col("R"), 15.0, None, ALU.is_equal, None, ["cR"])
+    mkcol("m15m", col("m15"), -1.0, None, ALU.add, None, ["cm15"])
+    for t in range(RO - 1):
+        mkcol("r%d" % t, col("R"), float(13 + t), None, ALU.is_equal, None, ["cR"])
+        mkcol("nr%d" % t, col("R"), float(13 + t), None, ALU.not_equal, None, ["cR"])
+    mkcol("d128", col("R"), 15.0, 128.0, ALU.is_lt, ALU.mult, ["cR"])
+    mkcol("x16", col("m15"), -16.0, None, ALU.mult, None, ["cm15"])
+    tt(newcol("RP"), col("R"), col("x16"), ALU.add, ["cR", "cx16"], ["cRP"], 1)
+    J1, JM1 = T.J[:, 0:128], T.JM[:, 0:128]
+    for u, h, n_ in ((0, 0, "P"), (1, 1, "P"), (0, 1, "Pp16"), (1, 0, "Pm16")):
+        nm = "SW%d%d" % (u, h)
+        ts(T[nm][:], J1, col(n_), col("U%d" % u), ALU.is_equal, ALU.mult, ["J", "c" + n_, "cU%d" % u], [nm])
+    ts(T.IDb[:], J1, col("P"), None, ALU.is_equal, None, ["J", "cP"], ["IDb"])
+    ts(T.BOb[:], T.JG[:], col("G"), None, ALU.is_equal, None, ["JG", "cG"], ["BOb"])
+    ts(T.ta[:, 0:128], JM1, 15.0, None, ALU.is_lt, None, ["JM"], ["ta0"])
+    tt(T.ZS[:], T.ta[:, 0:128], T.BOb[:], ALU.mult, ["ta0", "BOb"], ["ZS"], 128, 2)
+    ts(T.W1[:], T.J[:, 0:144], col("G15"), None, ALU.is_equal, None, ["J", "cG15"], ["W1"], 144)
+    ts(T.W2[:], T.J[:, 0:144], col("G15"), -2.0, ALU.is_equal, ALU.mult, ["J", "cG15"], ["W2"], 144)
+    ts(T.tb[:, 0:128], JM1, 15.0, -16.0, ALU.is_equal, ALU.mult, ["JM"], ["tb0"])
+    tt(T.JP[:], T.tb[:, 0:128], JM1, ALU.add, ["tb0", "JM"], ["JP"], 128, 2)
+    ts(T.ta[:, 128:256], T.JP[:], col("RP"), -2.0, ALU.is_lt, ALU.mult, ["JP", "cRP"], ["ta1"])
+    ts(T.tb[:, 128:256], T.JP[:], col("RP"), None, ALU.is_equal, None, ["JP", "cRP"], ["tb1"])
+    tt(T.tc[:, 0:128], T.ta[:, 128:256], T.tb[:, 128:256], ALU.add, ["ta1", "tb1"], ["tc0"], 128, 2)
+    tt(T.tc[:, 128:256], T.tc[:, 0:128], T.BOb[:], ALU.mult, ["tc0", "BOb"], ["tc1"], 128, 2)
+    for t in range(RO):
+        nm = "rv%d" % t
+        mkcol(nm, col("RP"), float(13 + t), None, ALU.is_lt, None, ["cRP"])
+        ts(T.td[:, 0:128], T.JP[:], float(13 + t), col(nm), ALU.is_lt, ALU.mult, ["JP", "c" + nm], ["td0"])
+        tt(T["TRI%d" % t][:], T.td[:, 0:128], T.tc[:, 128:256], ALU.mult, ["td0", "tc1"], ["TRI%d" % t], 128, 2)
+    ts(T.BOh[:], T.JG[:], col("G"), None, ALU.is_equal, None, ["JG", "cG"], ["BOh"])
+    ts(T.IDh[:], J1, col("P"), None, ALU.is_equal, None, ["J", "cP"], ["IDh"])
+    ts(T.ta[:], T.JM[:], col("R"), 8192.0 + CEN + 1, ALU.is_equal, ALU.mult, ["JM", "cR"], ["ta0", "ta1"], 256)
+    ts(T.MKl[:], T.ta[:], -8192.0, None, ALU.add, None, ["ta0", "ta1"], ["MKl"], 256)
+    ts(T.RS[:], T.JM[:], 0.0, None, ALU.is_gt, None, ["JM"], ["RS"], 256)
+    ts(T.tb[:, 0:128], JM1, col("R"), col("d128"), ALU.is_ge, ALU.mult, ["JM", "cR", "cd128"], ["tb0"])
+    tt(T.DEAD[:], T.tb[:, 0:128], T.ZS[:], ALU.mult, ["tb0", "ZS"], ["DEAD"], 128, 2)
+    stage[0] = 3
+    ts(T.tb[:, 128:256], JM1, col("R"), 8192.0, ALU.is_equal, ALU.mult, ["JM", "cR"], ["tb1"])
+    ts(T.MK0[:], T.tb[:, 128:256], -8192.0, None, ALU.add, None, ["tb1"], ["MK0"])
+    ts(T.MK2[:], T.JM[:], col("R"), float(B - 1), ALU.is_equal, ALU.mult, ["JM", "cR"], ["MK2"], 256)
+    ts(T.NBb[:], T.JG[:], col("G"), -float(2 ** 23), ALU.is_equal, ALU.mult, ["JG", "cG"], ["NBb"])
+    ts(T.FBb[:], T.JG[:], col("G"), 2.0 ** -10, ALU.is_equal, ALU.mult, ["JG", "cG"], ["FBb"])
+    ts(T.ta[:, 0:128], JM1, col("R"), -float(2 ** 23), ALU.is_gt, ALU.mult, ["JM", "cR"], ["ta0"])
+    ts(T.ta[:, 128:256], JM1, col("R"), 2.0 ** -10, ALU.is_le, ALU.mult, ["JM", "cR"], ["ta1"])
+    tt(T.td[:, 128:256], T.ta[:, 0:128], T.ta[:, 128:256], ALU.add, ["ta0", "ta1"], ["td1"], 128, 2)
+    tt(T.MTb[:], T.td[:, 128:256], T.BOb[:], ALU.mult, ["td1", "BOb"], ["MTb"], 128, 2)
+    for d, n1, n2 in (("1", "Pp16", "Pm112"), ("2", "Pp32", "Pm96"), ("3", "Pp48", "Pm80")):
+        ts(T.ta[:, 0:128], J1, col(n1), None, ALU.is_equal, None, ["J", "c" + n1], ["ta0"])
+        ts(T.tb[:, 0:128], J1, col(n2), None, ALU.is_equal, None, ["J", "c" + n2], ["tb0"])
+        tt(T["PM" + d][:], T.ta[:, 0:128], T.tb[:, 0:128], ALU.add, ["ta0", "tb0"], ["PM" + d], 128, 2)
+    for t in range(RO - 1):
+        ts(T["NW%d" % t][:], T.J[:], float(W0N + K * t), col("r%d" % t), ALU.add, ALU.mult, ["J", "cr%d" % t], ["NW%d" % t], 256)
+    ts(T.tb[:, 128:144], T.J[:, 0:16], 16.0, None, ALU.mult, None, ["J"], ["tb1"], 16)
+    ts(T.TR[:], T.tb[:, 128:144], col("R"), None, ALU.add, None, ["tb1", "cR"], ["TR"], 16)
+
+    def nlist(u):
+        return T.NL[:, 8 * u:8 * u + 8]
+
+    def xw(t):
+        return T.X[:, 0:B + W0N + K * t]
+
+    def aw(t):
+        return T.A[:, 0:B + W0N + K * t]
+
+    def prep(t, u):
+        s = str(u)
+        ts(T["AT" + s][:], aw(t).indirect(nlist(u)), float(-CEN), None, ALU.add, None, AK + ["NL" + s], ["AT" + s], 128, 1, GAT)
+        for b in range(4):
+            op("V", lambda b=b: g.vector.transpose(T["T1" + s][:, b:128:4], T["AT" + s][:, 32 * b:32 * b + 32]),
+               ["AT" + s], ["T1%s%d" % (s, b)], vd(32))
+        lst = []
+        for v in range(2):
+            for h in range(2):
+                lst.append((T["pc" + s][:, v:128:2], T["SW%d%d" % (v, h)][:], T["T1" + s][:, 64 * h:64 * h + 64], h == 0, h == 1))
+        mms(lst, ["T1%s%d" % (s, b) for b in range(4)] + ["SW00", "SW01", "SW10", "SW11"], ["pc" + s], 64)
+        n = 8 * (13 + t)
+        ts(T["LT" + s][:, 0:n], T["pc" + s][:, 0:n], float(CEN + B), None, ALU.add, None, ["pc" + s], ["LT" + s], n)
+
+    def bulk(t, u, step):
+        s = str(u)
+        nl = 13 + t
+        mms([(T["pz" + s][:, 128 * j:128 * j + 128], T.IDb[:], T["z" + s][:], True, True) for j in range(2)],
+            ["IDb", "z" + s], ["pz" + s])
+        pd = T["pd" + s][:, 0:128]
+        mms([(pd, T.ZS[:], T["z" + s][:], True, False)], ["ZS", "z" + s], ["pd" + s])
+        for k in range(step):
+            mms([(pd, T.DEAD[:], T["sel%d%s" % (k, s)][:], False, False)], ["DEAD", "sel%d%s" % (k, s)], ["pd" + s])
+        for a in range(0, nl, 2):
+            b = min(a + 2, nl)
+            n = 128 * (b - a)
+            h = slice(128 * a, 128 * b)
+            x, m = "xg%s%d" % (s, a), "mn%s%d" % (s, a)
+            act(T["xg" + s][:, h], xw(t).indirect(T["LT" + s][:, 8 * a:8 * b]), ACT.Identity, 160.0, 1.0, XK + ["LT" + s], [x], n, GAT)
+            tt(T["mn" + s][:, h], T["xg" + s][:, h], T["pz" + s][:, 0:n], ALU.min, [x, "pz" + s], [m], n)
+            mms([(pd, T.W1[:, 15 - i:143 - i], T["xg" + s][:, 128 * i:128 * i + 128], False, False) for i in range(a, b)],
+                ["W1", x], ["pd" + s])
+            mms([(pd, T.W2[:, 15 - i:143 - i], T["mn" + s][:, 128 * i:128 * i + 128], False, i == nl - 1) for i in range(a, b)],
+                ["W2", m], ["pd" + s])
+
+    def choose(t, u, step):
+        s = str(u)
+        k = "sel%d%s" % (step, s)
+        ts(T["ok" + s][:], T["pd" + s][:, 0:128], 68.0, None, ALU.is_lt, None, ["pd" + s], ["ok" + s])
+        mms([(T["pe" + s][:, 0:128], T["TRI%d" % t][:], T["ok" + s][:], True, True)], ["TRI%d" % t, "ok" + s], ["pe" + s])
+        ts(T[k][:], T["pe" + s][:, 0:128], 0.0, None, ALU.max, None, ["pe" + s], [k])
+        mms([(T["pc" + s][:, 0:128], T.IDh[:], T.MKl[:, 0:128], True, False)], ["IDh", "MKl"], ["pc" + s])
+        tt(T["sA" + s][:], T[k][:], T["AT" + s][:], ALU.mult, [k, "AT" + s], ["sA" + s], 128, 2)
+        mms([(T["pc" + s][:, 0:128], T.BOh[:], T["sA" + s][:], False, True)], ["BOh", "sA" + s], ["pc" + s])
+        scn(T["sc" + s][:], T["pc" + s][:, 0:128], 128, ["pc" + s], ["sc" + s])
+        ts(nlist(u), T["sc" + s][:, 15:128:16], float(B - 1), None, ALU.add, None, ["sc" + s], ["NL" + s], 8)
+
+    def advance(t, u):
+        s = str(u)
+        tt(T["s" + s][:], xw(t).indirect(nlist(u)), T["z" + s][:], ALU.add, XK + ["NL" + s, "z" + s], ["s" + s], 128, 1, GAT)
+        act(T["z" + s][:], T["s" + s][:], ACT.Identity, 79.75, 0.5, ["s" + s], ["z" + s])
+
+    peers = [T.cores[q] for q in range(len(T.cores)) if q != rank]
+
+    def finish(t, u):
+        s = str(u)
+        h = slice(128 * u, 128 * u + 128)
+        h8 = slice(8 * u, 8 * u + 8)
+        act(T.yg[:, h], xw(t).indirect(nlist(u)), ACT.Identity, 160.0, 1.0, XK + ["NL" + s], ["yg" + s], 128, GAT)
+        mms([(T["pc" + s][:, 128:256], T.BOh[:], T["sA" + s][:], True, True)], ["BOh", "sA" + s], ["pc" + s])
+        cp(T.vb[:, h], T["pc" + s][:, 128:256], ["pc" + s], ["vb" + s], 128)
+        ts(T.vT[:, h8], T["sc" + s][:, 15:128:16], float(-CEN - 1), None, ALU.add, None, ["sc" + s], ["vT" + s], 8)
+        ts(T.vX[:, h8], T["sc" + s][:, 15:128:16], float(B - 1), None, ALU.add, None, ["sc" + s], ["vX" + s], 8)
+        tt(T["gt" + s][:], T.yg[:, h], T["z" + s][:], ALU.is_gt, ["yg" + s, "z" + s], ["gt" + s], 128, 2)
+        o = T["pe" + s][:, 0:128]
+        mms([(o, T.IDh[:], T.MK0[:], True, False)], ["IDh", "MK0"], ["pe" + s])
+        mms([(o, T.BOb[:], T["gt" + s][:], False, True)], ["BOb", "gt" + s], ["pe" + s])
+        scn(T["sv" + s][:], o, 128, ["pe" + s], ["sv" + s])
+        ts(T.wt[:, h8], T["sv" + s][:, 15:128:16], 9.0, 2.0 ** -9, ALU.is_lt, ALU.add, ["sv" + s], ["wt" + s], 8)
+        tt(T["s2" + s][:], T.yg[:, h], T["z" + s][:], ALU.add, ["yg" + s, "z" + s], ["s2" + s], 128, 2)
+        act(T["z" + s][:], T["s2" + s][:], ACT.Identity, -0.25, 0.5, ["s2" + s], ["z" + s])
+        for b in range(2):
+            q = 2 * u + b
+            d = (q - rank) % len(T.cores)
+            zz = T["z" + s][:, 64 * b:64 * b + 64]
+            if d == 0:
+                c0 = B + W0N + K * t + 64 * rank
+                act(T.X[:, c0:c0 + 64], zz, ACT.Identity, -160.0, 1.0, ["z" + s], ["Xo%d" % t], 64)
+            else:
+                k = q if q < rank else q - 1
+                mms([(T["pz" + s][:, 64 * b:64 * b + 64], T["PM%d" % d][:], zz, True, True)], ["PM%d" % d, "z" + s], ["pz" + s], 64)
+                act(T.snd[:, 64 * k:64 * k + 64], T["pz" + s][:, 64 * b:64 * b + 64], ACT.Identity, -160.0, 1.0, ["pz" + s], ["snd%d" % k], 64)
+
+    def send(t):
+        used = []
+        trs = [None] * len(peers)
+        c0 = B + W0N + K * t + 64 * rank
+        for k in sorted(range(len(peers)), key=lambda k: topo.chip(peers[k]) == topo.chip(core)):
+            en = [e for e in topo.engines(core, peers[k]) if e not in used][:4]
+            used += en
+            rid, pid = topo.addr(peers[k])[:2]
+            trs[k] = RemoteDMATransfer(dst_ids=[DstId(rid=rid, pnc=pid)], dma_engine_mask=sum(1 << e for e in en),
+                                       remote_sem=T.sem["arr%d" % t], src=T.snd[:, 64 * k:64 * k + 64], dst=T.X[:, c0:c0 + 64])
+        rec("G", "send", lambda: g.remote_dma_fused(trs, local_sem=T.sem.snt), ["snd%d" % k for k in range(len(peers))],
+            ["Xa%d" % t], 1.5, 4.0, "arr%d" % t)
+
+    def pairs(k, c0, c1):
+        e = "EQ%d_%d" % (k, c0)
+        u = k // 8
+        ts(T.EQ[:, 256 * k + c0:256 * k + c1], T.vb[:, c0:c1], T.vT[:, k:k + 1], T.wt[:, k:k + 1], ALU.is_equal, ALU.mult,
+           ["vb%d" % v for v in range(c0 // 128, c1 // 128)] + ["vT%d" % u, "wt%d" % u], [e], c1 - c0, 0.5)
+        a, b = 16 * k, 16 * k + 16
+        lst = []
+        for lo, hi, m in ((c0, min(a, c1), "FBb"), (a, b, "MTb"), (max(b, c0), c1, "NBb")):
+            if lo < hi and lo >= c0 and hi <= c1:
+                lst.append((T.pd0[:, lo:hi], T[m][:], T.EQ[:, 256 * k + lo:256 * k + hi], False, k == 15 and m == "MTb"))
+        mms(lst, ["FBb", "MTb", "NBb", e], ["pd0"], (c1 - c0) / len(lst) + 32)
+
+    def joint(u):
+        s = str(u)
+        if u == 0:
+            mms([(T.pd0[:, 0:256], T.IDh[:], T.MKl[:], True, False), (T.pd0[:, 0:256], T.IDh[:], T.MK2[:], False, False)],
+                ["IDh", "MKl", "MK2"], ["pd0"], 256)
+        mms([(T.pd0[:, 128 * u:128 * u + 128], T.BOh[:], T["sA" + s][:], False, False)], ["BOh", "sA" + s], ["pd0"])
+
+    def settle(t):
+        scn(T.scL[:], T.pd0[:, 0:256], 256, ["pd0"], ["scL"])
+        f = T.scL[:, 15:256:16]
+        if t < RO - 1:
+            tt(T.ofs[:], f, T.TR[:], ALU.max, ["scL", "TR"], ["ofs"], 16, 2)
+            cp(T.OFF[:], T.ofs[:], ["ofs"], ["OFF"], 16)
+            cp(aw(t).indirect(T.OFF[:]), T.VA[:], ["VA", "OFF"], AK, 256, 3.0)
+        tt(T.fe[:], f, T.vX[:], ALU.subtract, ["scL", "vX0", "vX1"], ["fe"], 16, 2)
+        ts(T.ff[:], T.fe[:], 0.0007, None, ALU.is_lt, None, ["fe"], ["ff"], 16)
+        tt(T.fm[:], T.ff[:], f, ALU.mult, ["ff", "scL"], ["fm"], 16, 2)
+        tt(T.fo[:], T.fm[:], T.TR[:], ALU.max, ["fm", "TR"], ["fo"], 16, 2)
+        cp(T.OFX[:], T.fo[:], ["fo"], ["OFX"], 16)
+        cp(xw(t).indirect(T.OFX[:]), T.VX[:], ["VX", "OFX"], XK, 256, 3.0)
+
+    def newlinks(t):
+        ts(T.AF[:], aw(t).indirect(T.NL[:]), col("nr%d" % t), None, ALU.mult, None, AK + ["NL0", "NL1", "cnr%d" % t], ["AF"], 256, 1, GAT)
+        tt(T.VA[:], T.AF[:], T["NW%d" % t][:], ALU.add, ["AF", "NW%d" % t], ["VA"], 256, 2)
+        c0 = B + W0N + K * t
+        ts(T.A[:, c0:c0 + K], T.AF[:], col("m15"), col("m15m"), ALU.mult, ALU.add, ["AF", "cm15", "cm15m"], ["An%d" % t], 256)
+
+    for t in range(RO):
+        for u in range(2):
+            stage[0] = 10 * t + 1 + u
+            s = str(u)
+            act(T["z" + s][:], xw(max(t - 1, 0)).indirect(nlist(u)), ACT.Identity, 160.0, 1.0, XK + ["NL" + s], ["z" + s], 128, GAT)
+            prep(t, u)
+        if t:
+            XK = XK + ["Xa%d" % (t - 1), "Xo%d" % (t - 1)]
+        for st in range(S):
+            for u in range(2):
+                stage[0] = 10 * t + 1 + 2 * st + u
+                bulk(t, u, st)
+                choose(t, u, st)
+                if st < S - 1:
+                    prep(t, u)
+                    advance(t, u)
+                else:
+                    finish(t, u)
+                    joint(u)
+                    if u == 0:
+                        for k in range(8):
+                            pairs(k, 0, 128)
+        stage[0] = 10 * t + 9
+        send(t)
+        act(T.VX[:], T.yg[:], ACT.Identity, col("fb"), col("fs"), ["yg0", "yg1", "cfb", "cfs"], ["VX"], 256)
+        for k in range(8):
+            pairs(k, 128, 256)
+        for k in range(8, 16):
+            pairs(k, 0, 256)
+        if t < RO - 1:
+            newlinks(t)
+        else:
+            ts(T.vout[:], T.vb[:], float(CEN), None, ALU.add, None, ["vb0", "vb1"], ["vout"], 256)
+            dma("Y", T.yv[:], T.vout[0:128:16, :], "dO", ["vout"], [], 2.0)
+        settle(t)
+        if t < RO - 1:
+            AK = AK + ["An%d" % t]
+    XK = XK + ["Xa%d" % (RO - 1), "Xo%d" % (RO - 1)]
+    dma("Y", T.yx[:], T.X[:, B:B + W0N + RO * K], "dO", XK, [], 5.0)
+
+    n = len(recs)
+    preds = [set() for _ in range(n)]
+    lw, lr = {}, {}
+
+    def bank(k):
+        return k[0] == "p"
+
+    for i, r in enumerate(recs):
+        reads, writes = r[3], r[4]
+        for k in reads:
+            if k in lw:
+                preds[i].add(lw[k])
+            lr.setdefault(k, []).append(i)
+        for k in writes:
+            if k in lw:
+                preds[i].add(lw[k])
+            preds[i].update(lr.get(k, []))
+        for k in reads + writes:
+            if bank(k) or k in writes:
+                lw[k] = i
+                lr[k] = []
+        preds[i].discard(i)
+    succ = [[] for _ in range(n)]
+    for i in range(n):
+        for j in preds[i]:
+            succ[j].append(i)
+    prio = [0.0] * n
+    for i in range(n - 1, -1, -1):
+        prio[i] = recs[i][5] + recs[i][6] + max([prio[j] + WK for j in succ[i]], default=0.0)
+    left = [len(p) for p in preds]
+    ready = [0.0] * n
+    avail = {q: [] for q in QUE}
+    for i in range(n):
+        if left[i] == 0:
+            avail[recs[i][0]].append(i)
+    tq = {q: 0.0 for q in QUE}
+    order = []
+    while len(order) < n:
+        best = None
+        for q in QUE:
+            if avail[q]:
+                e = min(max(tq[q], ready[i]) for i in avail[q])
+                if best is None or e < best[0]:
+                    best = (e, q)
+        e, q = best
+        c = [i for i in avail[q] if max(tq[q], ready[i]) <= e + 0.02]
+        i = max(c, key=lambda j: (-recs[j][8], prio[j], -j))
+        avail[q].remove(i)
+        tq[q] = max(tq[q], ready[i]) + recs[i][5]
+        end = tq[q] + recs[i][6]
+        order.append(i)
+        for j in succ[i]:
+            same = recs[j][0] == q == "P"
+            ready[j] = max(ready[j], tq[q] if same else end + WK)
+            left[j] -= 1
+            if left[j] == 0:
+                avail[recs[j][0]].append(j)
+
+    cnt = {}
+    known = {q: {} for q in QUE}
+    lastw, lastr = {}, {}
+
+    def need(q, tok):
+        sem, val, clk = tok
+        kn = known[q]
+        if kn.get(sem, 0) >= val:
+            return
+        QUE[q].wait_ge(T.sem[sem], val)
+        kn[sem] = val
+        for s_, v_ in clk.items():
+            if kn.get(s_, 0) < v_:
+                kn[s_] = v_
+
+    total = {}
+    for r in recs:
+        if r[1] == "dma":
+            total[r[7]] = total.get(r[7], 0) + 16
+    for i in order:
+        q, kind, fn, reads, writes, dur, lat, sem, stg = recs[i]
+        toks = []
+        for k in reads:
+            if bank(k):
+                toks += [x for q2, x in lastr.get(k, {}).items() if q2 != q]
+            elif k in lastw:
+                toks.append(lastw[k])
+        for k in writes:
+            if k in lastw:
+                toks.append(lastw[k])
+            toks += [x for q2, x in lastr.get(k, {}).items() if q2 != q or not bank(k)]
+        for x in sorted(toks, key=lambda x: -x[1]):
+            need(q, x)
+        if kind == "op":
+            sm = "q" + q
+            cnt[sm] = cnt.get(sm, 0) + 1
+            fn().then_inc(T.sem[sm], 1)
+            tok = rtok = (sm, cnt[sm], dict(known[q]))
+            who = q
+        elif kind == "dma":
+            fn().then_inc(T.sem[sem], 16)
+            cnt[sem] = total[sem]
+            tok = rtok = (sem, total[sem], dict(known[q]) if total[sem] == 16 else {})
+            who = q + sem
+        else:
+            fn()
+            cnt["snt"] = cnt.get("snt", 0) + 4 * len(peers)
+            rtok = ("snt", cnt["snt"], dict(known[q]))
+            cnt[sem] = 4 * len(peers)
+            tok = (sem, cnt[sem], {})
+            who = "rem"
+        for k in writes:
+            if bank(k):
+                lastr.setdefault(k, {})[q] = tok
+            else:
+                lastw[k] = tok
+                lastr[k] = {}
+        for k in reads:
+            lastr.setdefault(k, {})[who] = rtok
+    for sem, val in cnt.items():
+        need("Y", (sem, val, {}))

@@ -6,14 +6,21 @@ ALU = AluOpType
 ACT = ActivationFunctionType
 
 W0N, K, RO, S = 3072, 256, 3, 4
+NU = 4
+W = K // NU
+WB = W // 16
 B = 272
 CEN = 1919
+NM = 15
+GC = 7
+MC = 256 // W
 XC = B + W0N + RO * K
 AC = B + W0N + (RO - 1) * K
 CYC = 0.00083
-PEC = 0.00055
-GAT = 1.45
-WK = 0.08
+PEC = 0.00045
+GAT = 1.4
+WK = 0.2
+LOOK = 0.02
 
 SCRATCH = {}
 
@@ -27,28 +34,21 @@ _b("A", AC, "int32")
 _b("WL", 16, "int32")
 for _n in ("NL", "OFF", "OFX"):
     _b(_n, 16, "uint16")
-for _u in "01":
-    for _n in ("z", "ok", "s", "gt"):
-        _b(_n + _u, 128, "bfloat16")
-    for _n in ("AT", "T1", "sA"):
-        _b(_n + _u, 128, "float16")
-    for _n in ("sc", "sv", "s2"):
-        _b(_n + _u, 128, "float32")
-    _b("LT" + _u, 128, "uint16")
-    _b("xg" + _u, 1920, "bfloat16")
-    _b("mn" + _u, 1920, "bfloat16")
-    for _s in "0123":
-        _b("sel" + _s + _u, 128, "bfloat16")
-    for _n in ("pz", "pd", "pc", "pe"):
-        _b(_n + _u, 512, "float32", "psum")
-_b("yg", 256, "bfloat16")
-_b("vb", 256, "float16")
-for _n in ("vT", "vX", "wt", "ofs", "fe", "ff", "fm", "fo", "TR"):
+for _n in ("z", "ok", "s", "gt", "yg", "sel0", "sel1", "sel2", "sel3", "VX"):
+    _b(_n, 256, "bfloat16")
+for _n in ("AT", "T1", "sA", "vb", "MKl", "MK2"):
+    _b(_n, 256, "float16")
+_b("LT", 256, "uint16")
+_b("xg", 15 * 256, "bfloat16")
+_b("mn", 15 * 256, "bfloat16")
+for _u in range(NU):
+    _b("pd%d" % _u, 512, "float32", "psum")
+    _b("pc%d" % _u, 512, "float32", "psum")
+for _n in ("vT", "vX", "wt", "ofs", "fd", "fe", "ff", "fm", "fo", "TR"):
     _b(_n, 16, "float32")
 _b("EQ", 16 * 256, "bfloat16")
-for _n in ("scL", "AF", "VA", "vout", "J", "JM", "ta", "tb", "tc", "td", "RS", "NW0", "NW1"):
+for _n in ("sc", "sv", "s2", "scL", "scM", "AF", "VA", "vout", "J", "JM", "ta", "tb", "tc", "td", "RS", "NW0", "NW1"):
     _b(_n, 256, "float32")
-_b("VX", 256, "bfloat16")
 _b("snd", 192, "bfloat16")
 _b("PI", 4, "int32")
 _b("col", 32, "float32")
@@ -60,8 +60,6 @@ for _n in ("BOb", "NBb", "FBb", "MTb", "ZS", "DEAD", "TRI0", "TRI1", "TRI2", "ID
     _b(_n, 128, "bfloat16")
 for _n in ("BOh", "IDh", "SW00", "SW01", "SW10", "SW11", "MK0"):
     _b(_n, 128, "float16")
-_b("MKl", 256, "float16")
-_b("MK2", 256, "float16")
 
 SEMAPHORES = ["qV", "qS", "qP", "qG", "dX", "dW", "dA", "dO", "arr0", "arr1", "arr2", "snt"]
 
@@ -110,7 +108,7 @@ def rank_program(g, core, T, topo):
             for (o, l, r_, st, sp) in lst:
                 r = g.tensor.matmul(o, l, r_, st, sp)
             return r
-        op("P", go, reads, writes, len(lst) * n * PEC)
+        op("P", go, reads, writes, len(lst) * max(n, 64) * PEC)
 
     dma("Y", T.WL[:], T.w0[:], "dW", [], ["WL"], 2.0)
     dma("Y", T.X[:, B:B + W0N], T.x0[:], "dX", [], ["X"], 5.0)
@@ -144,7 +142,7 @@ def rank_program(g, core, T, topo):
     def mkcol(name, in0, s1, s2, op0, op1, reads):
         ts(newcol(name), in0, s1, s2, op0, op1, reads, ["c" + name], 1)
 
-    ts(T.NL[:], T.WL[:], float(B), None, ALU.add, None, ["WL"], ["NL0", "NL1"], 16)
+    ts(T.NL[:], T.WL[:], float(B), None, ALU.add, None, ["WL"], ["NL%d" % u for u in range(NU)], 16)
     op("V", lambda: g.vector.memset(T.A[:, 0:B], -1), [], ["Am"], vd(B))
     op("V", lambda: g.vector.memset(T.X[:, 0:B], 95.0), [], ["Xm"], vd(B, 0.5))
     ts(T.PI[:, 1:2], T.PI[:, 0:1], 15, None, ALU.bitwise_and, None, ["PI"], ["PI1"], 1)
@@ -173,7 +171,7 @@ def rank_program(g, core, T, topo):
         ts(T[nm][:], J1, col(n_), col("U%d" % u), ALU.is_equal, ALU.mult, ["J", "c" + n_, "cU%d" % u], [nm])
     ts(T.IDb[:], J1, col("P"), None, ALU.is_equal, None, ["J", "cP"], ["IDb"])
     ts(T.BOb[:], T.JG[:], col("G"), None, ALU.is_equal, None, ["JG", "cG"], ["BOb"])
-    ts(T.ta[:, 0:128], JM1, 15.0, None, ALU.is_lt, None, ["JM"], ["ta0"])
+    ts(T.ta[:, 0:128], JM1, float(NM), None, ALU.is_lt, None, ["JM"], ["ta0"])
     tt(T.ZS[:], T.ta[:, 0:128], T.BOb[:], ALU.mult, ["ta0", "BOb"], ["ZS"], 128, 2)
     ts(T.W1[:], T.J[:, 0:144], col("G15"), None, ALU.is_equal, None, ["J", "cG15"], ["W1"], 144)
     ts(T.W2[:], T.J[:, 0:144], col("G15"), -2.0, ALU.is_equal, ALU.mult, ["J", "cG15"], ["W2"], 144)
@@ -194,8 +192,10 @@ def rank_program(g, core, T, topo):
     ts(T.MKl[:], T.ta[:], -8192.0, None, ALU.add, None, ["ta0", "ta1"], ["MKl"], 256)
     ts(T.RS[:], T.JM[:], 0.0, None, ALU.is_gt, None, ["JM"], ["RS"], 256)
     ts(T.tb[:, 0:128], JM1, col("R"), col("d128"), ALU.is_ge, ALU.mult, ["JM", "cR", "cd128"], ["tb0"])
-    tt(T.DEAD[:], T.tb[:, 0:128], T.ZS[:], ALU.mult, ["tb0", "ZS"], ["DEAD"], 128, 2)
-    stage[0] = 3
+    ts(T.tb[:, 128:256], JM1, 15.0, None, ALU.is_lt, None, ["JM"], ["tb1"])
+    tt(T.tc[:, 0:128], T.tb[:, 0:128], T.tb[:, 128:256], ALU.mult, ["tb0", "tb1"], ["tc0"], 128, 2)
+    tt(T.DEAD[:], T.tc[:, 0:128], T.BOb[:], ALU.mult, ["tc0", "BOb"], ["DEAD"], 128, 2)
+    stage[0] = 5
     ts(T.tb[:, 128:256], JM1, col("R"), 8192.0, ALU.is_equal, ALU.mult, ["JM", "cR"], ["tb1"])
     ts(T.MK0[:], T.tb[:, 128:256], -8192.0, None, ALU.add, None, ["tb1"], ["MK0"])
     ts(T.MK2[:], T.JM[:], col("R"), float(B - 1), ALU.is_equal, ALU.mult, ["JM", "cR"], ["MK2"], 256)
@@ -214,8 +214,23 @@ def rank_program(g, core, T, topo):
     ts(T.tb[:, 128:144], T.J[:, 0:16], 16.0, None, ALU.mult, None, ["J"], ["tb1"], 16)
     ts(T.TR[:], T.tb[:, 128:144], col("R"), None, ALU.add, None, ["tb1", "cR"], ["TR"], 16)
 
-    def nlist(u):
-        return T.NL[:, 8 * u:8 * u + 8]
+    def un(name, u):
+        return T[name][:, W * u:W * u + W]
+
+    def tab(name, u):
+        return T[name][:, WB * u:WB * u + WB]
+
+    def last16(name, u):
+        return T[name][:, W * u + 15:W * u + W:16]
+
+    def pz(u, n):
+        return T["pc%d" % u][:, 0:n]
+
+    def pe(u):
+        return T["pc%d" % u][:, 256:256 + W]
+
+    def pc(u):
+        return T["pc%d" % u][:, 384:384 + W]
 
     def xw(t):
         return T.X[:, 0:B + W0N + K * t]
@@ -225,86 +240,98 @@ def rank_program(g, core, T, topo):
 
     def prep(t, u):
         s = str(u)
-        ts(T["AT" + s][:], aw(t).indirect(nlist(u)), float(-CEN), None, ALU.add, None, AK + ["NL" + s], ["AT" + s], 128, 1, GAT)
-        for b in range(4):
-            op("V", lambda b=b: g.vector.transpose(T["T1" + s][:, b:128:4], T["AT" + s][:, 32 * b:32 * b + 32]),
-               ["AT" + s], ["T1%s%d" % (s, b)], vd(32))
+        ts(un("AT", u), aw(t).indirect(tab("NL", u)), float(-CEN), None, ALU.add, None, AK + ["NL" + s], ["AT" + s], W, 1, GAT)
+        nb = W // 32
+        o = W * u
+        for b in range(nb):
+            op("V", lambda b=b: g.vector.transpose(T.T1[:, o + b:o + W:nb] if nb > 1 else T.T1[:, o:o + W],
+                                                   T.AT[:, o + 32 * b:o + 32 * b + 32]), ["AT" + s], ["T1%s%d" % (s, b)], vd(32))
         lst = []
         for v in range(2):
             for h in range(2):
-                lst.append((T["pc" + s][:, v:128:2], T["SW%d%d" % (v, h)][:], T["T1" + s][:, 64 * h:64 * h + 64], h == 0, h == 1))
-        mms(lst, ["T1%s%d" % (s, b) for b in range(4)] + ["SW00", "SW01", "SW10", "SW11"], ["pc" + s], 64)
-        n = 8 * (13 + t)
-        ts(T["LT" + s][:, 0:n], T["pc" + s][:, 0:n], float(CEN + B), None, ALU.add, None, ["pc" + s], ["LT" + s], n)
+                lst.append((T["pc" + s][:, 384 + v:384 + W:2], T["SW%d%d" % (v, h)][:],
+                            T.T1[:, o + W // 2 * h:o + W // 2 * h + W // 2], h == 0, h == 1))
+        mms(lst, ["T1%s%d" % (s, b) for b in range(nb)] + ["SW00", "SW01", "SW10", "SW11"], ["pc" + s], W // 2)
+        n = WB * (13 + t)
+        ts(T.LT[:, o:o + n], T["pc" + s][:, 384:384 + n], float(CEN + B), None, ALU.add, None, ["pc" + s], ["LT" + s], n)
 
     def bulk(t, u, step):
         s = str(u)
         nl = 13 + t
-        mms([(T["pz" + s][:, 128 * j:128 * j + 128], T.IDb[:], T["z" + s][:], True, True) for j in range(2)],
-            ["IDb", "z" + s], ["pz" + s])
-        pd = T["pd" + s][:, 0:128]
-        mms([(pd, T.ZS[:], T["z" + s][:], True, False)], ["ZS", "z" + s], ["pd" + s])
+        o = 15 * W * u
+        pd = T["pd" + s][:, 0:W]
+        mms([(T["pc" + s][:, W * j:W * j + W], T.IDb[:], un("z", u), True, True) for j in range(MC)], ["IDb", "z" + s], ["pc" + s], W)
+        mms([(pd, T.ZS[:], un("z", u), True, False)], ["ZS", "z" + s], ["pd" + s], W)
         for k in range(step):
-            mms([(pd, T.DEAD[:], T["sel%d%s" % (k, s)][:], False, False)], ["DEAD", "sel%d%s" % (k, s)], ["pd" + s])
-        for a in range(0, nl, 2):
-            b = min(a + 2, nl)
-            n = 128 * (b - a)
-            h = slice(128 * a, 128 * b)
-            x, m = "xg%s%d" % (s, a), "mn%s%d" % (s, a)
-            act(T["xg" + s][:, h], xw(t).indirect(T["LT" + s][:, 8 * a:8 * b]), ACT.Identity, 160.0, 1.0, XK + ["LT" + s], [x], n, GAT)
-            tt(T["mn" + s][:, h], T["xg" + s][:, h], T["pz" + s][:, 0:n], ALU.min, [x, "pz" + s], [m], n)
-            mms([(pd, T.W1[:, 15 - i:143 - i], T["xg" + s][:, 128 * i:128 * i + 128], False, False) for i in range(a, b)],
-                ["W1", x], ["pd" + s])
-            mms([(pd, T.W2[:, 15 - i:143 - i], T["mn" + s][:, 128 * i:128 * i + 128], False, i == nl - 1) for i in range(a, b)],
-                ["W2", m], ["pd" + s])
+            mms([(pd, T.DEAD[:], un("sel%d" % k, u), False, False)], ["DEAD", "sel%d%s" % (k, s)], ["pd" + s], W)
+        n2 = min(NM, nl)
+        for a in range(0, n2, GC):
+            b = min(a + GC, n2)
+            x = "xg%s%d" % (s, a)
+            act(T.xg[:, o + W * a:o + W * b], xw(t).indirect(T.LT[:, W * u + WB * a:W * u + WB * b]), ACT.Identity, 160.0, 1.0,
+                XK + ["LT" + s], [x], W * (b - a), GAT)
+            for c in range(a, b, MC):
+                d = min(c + MC, b)
+                h = slice(o + W * c, o + W * d)
+                m = "mn%s%d" % (s, c)
+                tt(T.mn[:, h], T.xg[:, h], pz(u, W * (d - c)), ALU.min, [x, "pc" + s], [m], W * (d - c))
+                mms([(pd, T.W1[:, 15 - i:143 - i], T.xg[:, o + W * i:o + W * i + W], False, False) for i in range(c, d)],
+                    ["W1", x], ["pd" + s], W)
+                mms([(pd, T.W2[:, 15 - i:143 - i], T.mn[:, o + W * i:o + W * i + W], False, i == nl - 1) for i in range(c, d)],
+                    ["W2", m], ["pd" + s], W)
+        for i in range(n2, nl):
+            h = slice(o + W * i, o + W * i + W)
+            x, m = "xg%s%d" % (s, i), "mn%s%d" % (s, i)
+            tt(T.xg[:, h], xw(t).indirect(T.LT[:, W * u + WB * i:W * u + WB * i + WB]), un("z", u), ALU.subtract,
+               XK + ["LT" + s, "z" + s], [x], W, 1, GAT)
+            act(T.mn[:, h], T.xg[:, h], ACT.Abs, 160.0, 1.0, [x], [m], W)
+            mms([(pd, T.W1[:, 15 - i:143 - i], T.mn[:, h], False, i == nl - 1)], ["W1", m], ["pd" + s], W)
 
     def choose(t, u, step):
         s = str(u)
-        k = "sel%d%s" % (step, s)
-        ts(T["ok" + s][:], T["pd" + s][:, 0:128], 68.0, None, ALU.is_lt, None, ["pd" + s], ["ok" + s])
-        mms([(T["pe" + s][:, 0:128], T["TRI%d" % t][:], T["ok" + s][:], True, True)], ["TRI%d" % t, "ok" + s], ["pe" + s])
-        ts(T[k][:], T["pe" + s][:, 0:128], 0.0, None, ALU.max, None, ["pe" + s], [k])
-        mms([(T["pc" + s][:, 0:128], T.IDh[:], T.MKl[:, 0:128], True, False)], ["IDh", "MKl"], ["pc" + s])
-        tt(T["sA" + s][:], T[k][:], T["AT" + s][:], ALU.mult, [k, "AT" + s], ["sA" + s], 128, 2)
-        mms([(T["pc" + s][:, 0:128], T.BOh[:], T["sA" + s][:], False, True)], ["BOh", "sA" + s], ["pc" + s])
-        scn(T["sc" + s][:], T["pc" + s][:, 0:128], 128, ["pc" + s], ["sc" + s])
-        ts(nlist(u), T["sc" + s][:, 15:128:16], float(B - 1), None, ALU.add, None, ["sc" + s], ["NL" + s], 8)
+        k = "sel%d" % step
+        ts(un("ok", u), T["pd" + s][:, 0:W], 68.0, None, ALU.is_lt, None, ["pd" + s], ["ok" + s], W)
+        mms([(pe(u), T["TRI%d" % t][:], un("ok", u), True, True)], ["TRI%d" % t, "ok" + s], ["pc" + s], W)
+        ts(un(k, u), pe(u), 0.0, None, ALU.max, None, ["pc" + s], [k + s], W)
+        mms([(pc(u), T.IDh[:], T.MKl[:, 0:W], True, False)], ["IDh", "MKl"], ["pc" + s], W)
+        tt(un("sA", u), un(k, u), un("AT", u), ALU.mult, [k + s, "AT" + s], ["sA" + s], W, 2)
+        mms([(pc(u), T.BOh[:], un("sA", u), False, True)], ["BOh", "sA" + s], ["pc" + s], W)
+        scn(un("sc", u), pc(u), W, ["pc" + s], ["sc" + s])
+        ts(tab("NL", u), last16("sc", u), float(B - 1), None, ALU.add, None, ["sc" + s], ["NL" + s], WB)
 
     def advance(t, u):
         s = str(u)
-        tt(T["s" + s][:], xw(t).indirect(nlist(u)), T["z" + s][:], ALU.add, XK + ["NL" + s, "z" + s], ["s" + s], 128, 1, GAT)
-        act(T["z" + s][:], T["s" + s][:], ACT.Identity, 79.75, 0.5, ["s" + s], ["z" + s])
+        tt(un("s", u), xw(t).indirect(tab("NL", u)), un("z", u), ALU.add, XK + ["NL" + s, "z" + s], ["s" + s], W, 1, GAT)
+        act(un("z", u), un("s", u), ACT.Identity, 79.75, 0.5, ["s" + s], ["z" + s], W)
 
     peers = [T.cores[q] for q in range(len(T.cores)) if q != rank]
 
     def finish(t, u):
         s = str(u)
-        h = slice(128 * u, 128 * u + 128)
-        h8 = slice(8 * u, 8 * u + 8)
-        act(T.yg[:, h], xw(t).indirect(nlist(u)), ACT.Identity, 160.0, 1.0, XK + ["NL" + s], ["yg" + s], 128, GAT)
-        mms([(T["pc" + s][:, 128:256], T.BOh[:], T["sA" + s][:], True, True)], ["BOh", "sA" + s], ["pc" + s])
-        cp(T.vb[:, h], T["pc" + s][:, 128:256], ["pc" + s], ["vb" + s], 128)
-        ts(T.vT[:, h8], T["sc" + s][:, 15:128:16], float(-CEN - 1), None, ALU.add, None, ["sc" + s], ["vT" + s], 8)
-        ts(T.vX[:, h8], T["sc" + s][:, 15:128:16], float(B - 1), None, ALU.add, None, ["sc" + s], ["vX" + s], 8)
-        tt(T["gt" + s][:], T.yg[:, h], T["z" + s][:], ALU.is_gt, ["yg" + s, "z" + s], ["gt" + s], 128, 2)
-        o = T["pe" + s][:, 0:128]
-        mms([(o, T.IDh[:], T.MK0[:], True, False)], ["IDh", "MK0"], ["pe" + s])
-        mms([(o, T.BOb[:], T["gt" + s][:], False, True)], ["BOb", "gt" + s], ["pe" + s])
-        scn(T["sv" + s][:], o, 128, ["pe" + s], ["sv" + s])
-        ts(T.wt[:, h8], T["sv" + s][:, 15:128:16], 9.0, 2.0 ** -9, ALU.is_lt, ALU.add, ["sv" + s], ["wt" + s], 8)
-        tt(T["s2" + s][:], T.yg[:, h], T["z" + s][:], ALU.add, ["yg" + s, "z" + s], ["s2" + s], 128, 2)
-        act(T["z" + s][:], T["s2" + s][:], ACT.Identity, -0.25, 0.5, ["s2" + s], ["z" + s])
-        for b in range(2):
-            q = 2 * u + b
+        act(un("yg", u), xw(t).indirect(tab("NL", u)), ACT.Identity, 160.0, 1.0, XK + ["NL" + s], ["yg" + s], W, GAT)
+        mms([(pe(u), T.BOh[:], un("sA", u), True, True)], ["BOh", "sA" + s], ["pc" + s], W)
+        cp(un("vb", u), pe(u), ["pc" + s], ["vb" + s], W)
+        ts(tab("vT", u), last16("sc", u), float(-CEN - 1), None, ALU.add, None, ["sc" + s], ["vT" + s], WB)
+        ts(tab("vX", u), last16("sc", u), float(B + CEN), None, ALU.add, None, ["sc" + s], ["vX" + s], WB)
+        tt(un("gt", u), un("yg", u), un("z", u), ALU.is_gt, ["yg" + s, "z" + s], ["gt" + s], W, 2)
+        mms([(pc(u), T.IDh[:], T.MK0[:, 0:W], True, False)], ["IDh", "MK0"], ["pc" + s], W)
+        mms([(pc(u), T.BOb[:], un("gt", u), False, True)], ["BOb", "gt" + s], ["pc" + s], W)
+        scn(un("sv", u), pc(u), W, ["pc" + s], ["sv" + s])
+        ts(tab("wt", u), last16("sv", u), 9.0, 2.0 ** -9, ALU.is_lt, ALU.add, ["sv" + s], ["wt" + s], WB)
+        tt(un("s2", u), un("yg", u), un("z", u), ALU.add, ["yg" + s, "z" + s], ["s2" + s], W, 2)
+        act(un("z", u), un("s2", u), ACT.Identity, -0.25, 0.5, ["s2" + s], ["z" + s], W)
+        for b in range(W // 64):
+            q = W // 64 * u + b
             d = (q - rank) % len(T.cores)
-            zz = T["z" + s][:, 64 * b:64 * b + 64]
+            zz = T.z[:, 64 * q:64 * q + 64]
             if d == 0:
                 c0 = B + W0N + K * t + 64 * rank
                 act(T.X[:, c0:c0 + 64], zz, ACT.Identity, -160.0, 1.0, ["z" + s], ["Xo%d" % t], 64)
             else:
                 k = q if q < rank else q - 1
-                mms([(T["pz" + s][:, 64 * b:64 * b + 64], T["PM%d" % d][:], zz, True, True)], ["PM%d" % d, "z" + s], ["pz" + s], 64)
-                act(T.snd[:, 64 * k:64 * k + 64], T["pz" + s][:, 64 * b:64 * b + 64], ACT.Identity, -160.0, 1.0, ["pz" + s], ["snd%d" % k], 64)
+                pp = T["pc" + s][:, 64 * b:64 * b + 64]
+                mms([(pp, T["PM%d" % d][:], zz, True, True)], ["PM%d" % d, "z" + s], ["pc" + s], 64)
+                act(T.snd[:, 64 * k:64 * k + 64], pp, ACT.Identity, -160.0, 1.0, ["pc" + s], ["snd%d" % k], 64)
 
     def send(t):
         used = []
@@ -320,32 +347,51 @@ def rank_program(g, core, T, topo):
             ["Xa%d" % t], 1.5, 4.0, "arr%d" % t)
 
     def pairs(k, c0, c1):
-        e = "EQ%d_%d" % (k, c0)
-        u = k // 8
+        u = k // WB
         ts(T.EQ[:, 256 * k + c0:256 * k + c1], T.vb[:, c0:c1], T.vT[:, k:k + 1], T.wt[:, k:k + 1], ALU.is_equal, ALU.mult,
-           ["vb%d" % v for v in range(c0 // 128, c1 // 128)] + ["vT%d" % u, "wt%d" % u], [e], c1 - c0, 0.5)
+           ["vb%d" % v for v in range(c0 // W, c1 // W)] + ["vT%d" % u, "wt%d" % u], ["EQ%d_%d" % (k, c0)], c1 - c0, 0.5)
+
+    def sums(ps, k, c0, c1, mats, last=False):
         a, b = 16 * k, 16 * k + 16
         lst = []
+        nn = 0
         for lo, hi, m in ((c0, min(a, c1), "FBb"), (a, b, "MTb"), (max(b, c0), c1, "NBb")):
-            if lo < hi and lo >= c0 and hi <= c1:
-                lst.append((T.pd0[:, lo:hi], T[m][:], T.EQ[:, 256 * k + lo:256 * k + hi], False, k == 15 and m == "MTb"))
-        mms(lst, ["FBb", "MTb", "NBb", e], ["pd0"], (c1 - c0) / len(lst) + 32)
+            if lo < hi and lo >= c0 and hi <= c1 and m in mats:
+                lst.append((T[ps][:, lo:hi], T[m][:], T.EQ[:, 256 * k + lo:256 * k + hi], False, last))
+                nn += max(64, hi - lo)
+        if lst:
+            mms(lst, list(mats) + ["EQ%d_%d" % (k, c0)], [ps], nn / len(lst))
 
     def joint(u):
         s = str(u)
         if u == 0:
             mms([(T.pd0[:, 0:256], T.IDh[:], T.MKl[:], True, False), (T.pd0[:, 0:256], T.IDh[:], T.MK2[:], False, False)],
                 ["IDh", "MKl", "MK2"], ["pd0"], 256)
-        mms([(T.pd0[:, 128 * u:128 * u + 128], T.BOh[:], T["sA" + s][:], False, False)], ["BOh", "sA" + s], ["pd0"])
+        mms([(T.pd0[:, W * u:W * u + W], T.BOh[:], un("sA", u), False, False)], ["BOh", "sA" + s], ["pd0"], W)
+        for k in range(WB * u):
+            pairs(k, W * u, W * u + W)
+            sums("pd0", k, W * u, W * u + W, ("NBb",))
+        for k in range(WB * u, WB * u + WB):
+            pairs(k, 0, W * u + W)
+            if u < NU - 1:
+                sums("pd0", k, 0, W * u + W, ("FBb", "MTb", "NBb"))
+            else:
+                sums("pd0", k, 0, K, ("MTb", "NBb"), k == 15)
 
     def settle(t):
-        scn(T.scL[:], T.pd0[:, 0:256], 256, ["pd0"], ["scL"])
         f = T.scL[:, 15:256:16]
+        scn(T.scL[:], T.pd0[:, 0:256], 256, ["pd0"], ["scL"])
         if t < RO - 1:
             tt(T.ofs[:], f, T.TR[:], ALU.max, ["scL", "TR"], ["ofs"], 16, 2)
             cp(T.OFF[:], T.ofs[:], ["ofs"], ["OFF"], 16)
             cp(aw(t).indirect(T.OFF[:]), T.VA[:], ["VA", "OFF"], AK, 256, 3.0)
-        tt(T.fe[:], f, T.vX[:], ALU.subtract, ["scL", "vX0", "vX1"], ["fe"], 16, 2)
+        stage[0] = 20 * t + 17.5
+        mms([(T.pd1[:, 0:256], T.IDh[:], T.MKl[:], True, False)], ["IDh", "MKl"], ["pd1"], 256)
+        for k in range(16 - WB, 16):
+            sums("pd1", k, 0, 256, ("FBb",), k == 15)
+        tt(T.fd[:], f, T.vX[:], ALU.subtract, ["scL"] + ["vX%d" % u for u in range(NU)], ["fd"], 16, 2)
+        scn(T.scM[:], T.pd1[:, 0:256], 256, ["pd1"], ["scM"])
+        tt(T.fe[:], T.fd[:], T.scM[:, 15:256:16], ALU.add, ["fd", "scM"], ["fe"], 16, 2)
         ts(T.ff[:], T.fe[:], 0.0007, None, ALU.is_lt, None, ["fe"], ["ff"], 16)
         tt(T.fm[:], T.ff[:], f, ALU.mult, ["ff", "scL"], ["fm"], 16, 2)
         tt(T.fo[:], T.fm[:], T.TR[:], ALU.max, ["fm", "TR"], ["fo"], 16, 2)
@@ -353,22 +399,23 @@ def rank_program(g, core, T, topo):
         cp(xw(t).indirect(T.OFX[:]), T.VX[:], ["VX", "OFX"], XK, 256, 3.0)
 
     def newlinks(t):
-        ts(T.AF[:], aw(t).indirect(T.NL[:]), col("nr%d" % t), None, ALU.mult, None, AK + ["NL0", "NL1", "cnr%d" % t], ["AF"], 256, 1, GAT)
+        ts(T.AF[:], aw(t).indirect(T.NL[:]), col("nr%d" % t), None, ALU.mult, None,
+           AK + ["NL%d" % u for u in range(NU)] + ["cnr%d" % t], ["AF"], 256, 1, GAT)
         tt(T.VA[:], T.AF[:], T["NW%d" % t][:], ALU.add, ["AF", "NW%d" % t], ["VA"], 256, 2)
         c0 = B + W0N + K * t
         ts(T.A[:, c0:c0 + K], T.AF[:], col("m15"), col("m15m"), ALU.mult, ALU.add, ["AF", "cm15", "cm15m"], ["An%d" % t], 256)
 
     for t in range(RO):
-        for u in range(2):
-            stage[0] = 10 * t + 1 + u
+        for u in range(NU):
+            stage[0] = 20 * t + 1 + u
             s = str(u)
-            act(T["z" + s][:], xw(max(t - 1, 0)).indirect(nlist(u)), ACT.Identity, 160.0, 1.0, XK + ["NL" + s], ["z" + s], 128, GAT)
+            act(un("z", u), xw(max(t - 1, 0)).indirect(tab("NL", u)), ACT.Identity, 160.0, 1.0, XK + ["NL" + s], ["z" + s], W, GAT)
             prep(t, u)
         if t:
             XK = XK + ["Xa%d" % (t - 1), "Xo%d" % (t - 1)]
         for st in range(S):
-            for u in range(2):
-                stage[0] = 10 * t + 1 + 2 * st + u
+            for u in range(NU):
+                stage[0] = 20 * t + 1 + NU * st + u
                 bulk(t, u, st)
                 choose(t, u, st)
                 if st < S - 1:
@@ -376,21 +423,15 @@ def rank_program(g, core, T, topo):
                     advance(t, u)
                 else:
                     finish(t, u)
+                    stage[0] = 20 * t + 16.5
                     joint(u)
-                    if u == 0:
-                        for k in range(8):
-                            pairs(k, 0, 128)
-        stage[0] = 10 * t + 9
+        stage[0] = 20 * t + 17
         send(t)
-        act(T.VX[:], T.yg[:], ACT.Identity, col("fb"), col("fs"), ["yg0", "yg1", "cfb", "cfs"], ["VX"], 256)
-        for k in range(8):
-            pairs(k, 128, 256)
-        for k in range(8, 16):
-            pairs(k, 0, 256)
+        act(T.VX[:], T.yg[:], ACT.Identity, col("fb"), col("fs"), ["yg%d" % u for u in range(NU)] + ["cfb", "cfs"], ["VX"], 256)
         if t < RO - 1:
             newlinks(t)
         else:
-            ts(T.vout[:], T.vb[:], float(CEN), None, ALU.add, None, ["vb0", "vb1"], ["vout"], 256)
+            ts(T.vout[:], T.vb[:], float(CEN), None, ALU.add, None, ["vb%d" % u for u in range(NU)], ["vout"], 256)
             dma("Y", T.yv[:], T.vout[0:128:16, :], "dO", ["vout"], [], 2.0)
         settle(t)
         if t < RO - 1:
@@ -443,7 +484,7 @@ def rank_program(g, core, T, topo):
                 if best is None or e < best[0]:
                     best = (e, q)
         e, q = best
-        c = [i for i in avail[q] if max(tq[q], ready[i]) <= e + 0.02]
+        c = [i for i in avail[q] if max(tq[q], ready[i]) <= e + LOOK]
         i = max(c, key=lambda j: (-recs[j][8], prio[j], -j))
         avail[q].remove(i)
         tq[q] = max(tq[q], ready[i]) + recs[i][5]

import numpy as np
from concourse.bass import DstId, RemoteDMATransfer
from concourse.mybir import AluOpType, ActivationFunctionType

ALU = AluOpType
ACT = ActivationFunctionType

W0N, K, RO, S = 3072, 256, 3, 4
NU = 4
W = K // NU
WB = W // 16
B = 272
CEN = 1919
NM = 15
GC = 7
MC = 256 // W
XC = B + W0N + RO * K
AC = B + W0N + (RO - 1) * K
CYC = 0.00083
PEC = 0.00045
GAT = 1.4
WK = 0.2
LOOK = 0.02

SCRATCH = {}


def _b(name, cols, dtype, where="sbuf"):
    SCRATCH[name] = (where, [128, cols], dtype)


_b("X", XC, "bfloat16")
_b("A", AC, "int32")
_b("WL", 16, "int32")
for _n in ("NL", "OFF", "OFX"):
    _b(_n, 16, "uint16")
for _n in ("z", "ok", "s", "gt", "yg", "sel0", "sel1", "sel2", "sel3", "VX"):
    _b(_n, 256, "bfloat16")
for _n in ("AT", "T1", "sA", "vb", "MKl", "MK2"):
    _b(_n, 256, "float16")
_b("LT", 256, "uint16")
_b("xg", 15 * 256, "bfloat16")
_b("mn", 15 * 256, "bfloat16")
for _u in range(NU):
    _b("pd%d" % _u, 512, "float32", "psum")
    _b("pc%d" % _u, 512, "float32", "psum")
for _n in ("vT", "vX", "wt", "ofs", "fd", "fe", "ff", "fm", "fo", "TR"):
    _b(_n, 16, "float32")
_b("EQ", 16 * 256, "bfloat16")
for _n in ("sc", "sv", "s2", "scL", "scM", "AF", "VA", "vout", "J", "JM", "ta", "tb", "tc", "td", "RS", "NW0", "NW1"):
    _b(_n, 256, "float32")
_b("snd", 192, "bfloat16")
_b("PI", 4, "int32")
_b("col", 32, "float32")
_b("JG", 128, "float32")
_b("JP", 128, "float32")
_b("W1", 144, "bfloat16")
_b("W2", 144, "bfloat16")
for _n in ("BOb", "NBb", "FBb", "MTb", "ZS", "DEAD", "TRI0", "TRI1", "TRI2", "IDb", "PM1", "PM2", "PM3"):
    _b(_n, 128, "bfloat16")
for _n in ("BOh", "IDh", "SW00", "SW01", "SW10", "SW11", "MK0"):
    _b(_n, 128, "float16")

SEMAPHORES = ["qV", "qS", "qP", "qG", "dX", "dW", "dA", "dO", "arr0", "arr1", "arr2", "snt"]


def rank_program(g, core, T, topo):
    rank = T.rank_of(core)
    if rank is None:
        return
    QUE = {"V": g.vector, "S": g.scalar, "P": g.tensor, "G": g, "Y": g.sync}
    recs = []
    stage = [0]

    def rec(q, kind, fn, reads, writes, dur, lat=0.0, sem=None):
        recs.append((q, kind, fn, tuple(reads), tuple(writes), dur, lat, sem, stage[0]))

    def op(q, fn, reads, writes, dur):
        rec(q, "op", fn, reads, writes, dur)

    def dma(q, out, in_, sem, reads, writes, lat):
        rec(q, "dma", lambda: QUE[q].dma_start(out, in_), reads, writes, 0.06, lat, sem)

    def vd(n, f=1.0, ind=None):
        return max(64, n * f) * CYC if ind is None else 0.05 + n * CYC * ind

    def ts(out, in0, s1, s2, op0, op1, reads, writes, n=128, f=1.0, ind=None):
        if op1 is None:
            op("V", lambda: g.vector.tensor_scalar(out, in0, s1, s2, op0), reads, writes, vd(n, f, ind))
        else:
            op("V", lambda: g.vector.tensor_scalar(out, in0, s1, s2, op0, op1), reads, writes, vd(n, f, ind))

    def tt(out, in0, in1, o, reads, writes, n=128, f=1.0, ind=None):
        op("V", lambda: g.vector.tensor_tensor(out, in0, in1, o), reads, writes, vd(n, f, ind))

    def cp(out, in_, reads, writes, n, ind=None):
        op("V", lambda: g.vector.tensor_copy(out, in_), reads, writes, vd(n, 1.0, ind))

    def act(out, in_, f, bias, scale, reads, writes, n=128, ind=1.0):
        op("S", lambda: g.scalar.activation(out, in_, f, bias=bias, scale=scale), reads, writes, 0.065 + n * CYC * ind)

    def scn(out, data1, n, reads, writes):
        op("V", lambda: g.vector.tensor_tensor_scan(out, T.RS[:, 0:n], data1, 0.0, ALU.mult, ALU.max), ["RS"] + reads, writes, vd(n))

    def mms(lst, reads, writes, n=128):
        def go():
            r = None
            for (o, l, r_, st, sp) in lst:
                r = g.tensor.matmul(o, l, r_, st, sp)
            return r
        op("P", go, reads, writes, len(lst) * max(n, 64) * PEC)

    dma("Y", T.WL[:], T.w0[:], "dW", [], ["WL"], 2.0)
    dma("Y", T.X[:, B:B + W0N], T.x0[:], "dX", [], ["X"], 5.0)
    for gr in range(8):
        dma("S" if gr % 2 == 0 else "Y", T.A[16 * gr:16 * gr + 15, B:B + W0N], T.lk[16 * gr:16 * gr + 15, :], "dA", [], ["A%d" % gr], 9.0)
    dma("S", T.A[15:128:16, B:B + W0N], T.nx[:], "dA", [], ["A8"], 9.0)
    AK = ["A%d" % i for i in range(9)] + ["Am"]
    XK = ["X", "Xm"]

    CI = {}

    def newcol(name):
        CI[name] = len(CI)
        return col(name)

    def col(name):
        i = CI[name]
        return T.col[:, i:i + 1]

    def iota(ap, key, pattern, base, cm, n, whole=False):
        if whole:
            op("G", lambda: g.iota(ap, pattern, base, cm), [], [key], 0.13 + 2 * CYC * n)
        else:
            op("G", lambda: g.iota(ap, pattern, base, cm, allow_small_or_imprecise_dtypes=True), [], [key], 0.13 + 2 * CYC * n)

    iota(T.PI[:, 0:1], "PI", [[0, 1]], 0, 1, 1, True)
    iota(T.JG[:], "JG", [[16, 8], [0, 16]], 0, 0, 128)
    iota(T.J[:], "J", [[1, 256]], 0, 0, 256)
    iota(T.JM[:], "JM", [[0, 16], [1, 16]], 0, 0, 256)

    def mkcol(name, in0, s1, s2, op0, op1, reads):
        ts(newcol(name), in0, s1, s2, op0, op1, reads, ["c" + name], 1)

    ts(T.NL[:], T.WL[:], float(B), None, ALU.add, None, ["WL"], ["NL%d" % u for u in range(NU)], 16)
    op("V", lambda: g.vector.memset(T.A[:, 0:B], -1), [], ["Am"], vd(B))
    op("V", lambda: g.vector.memset(T.X[:, 0:B], 95.0), [], ["Xm"], vd(B, 0.5))
    ts(T.PI[:, 1:2], T.PI[:, 0:1], 15, None, ALU.bitwise_and, None, ["PI"], ["PI1"], 1)
    ts(T.PI[:, 2:3], T.PI[:, 0:1], 16, None, ALU.bitwise_and, None, ["PI"], ["PI2"], 1)
    ts(T.PI[:, 3:4], T.PI[:, 0:1], 1, None, ALU.bitwise_and, None, ["PI"], ["PI3"], 1)
    for n_, a in (("P", 0), ("Pm16", -16), ("Pp16", 16), ("Pp32", 32), ("Pp48", 48), ("Pm112", -112), ("Pm96", -96), ("Pm80", -80)):
        mkcol(n_, T.PI[:, 0:1], float(a), None, ALU.add, None, ["PI"])
    mkcol("R", T.PI[:, 1:2], 0.0, None, ALU.add, None, ["PI1"])
    mkcol("U1", T.PI[:, 2:3], 0.0625, None, ALU.mult, None, ["PI2"])
    mkcol("U0", T.PI[:, 2:3], -0.0625, 1.0, ALU.mult, ALU.add, ["PI2"])
    mkcol("fs", T.PI[:, 3:4], 2.0, -1.0, ALU.mult, ALU.add, ["PI3"])
    mkcol("fb", T.PI[:, 3:4], -335.0, 175.0, ALU.mult, ALU.add, ["PI3"])
    tt(newcol("G"), col("P"), col("R"), ALU.subtract, ["cP", "cR"], ["cG"], 1)
    mkcol("G15", col("G"), 15.0, None, ALU.add, None, ["cG"])
    mkcol("m15", col("R"), 15.0, None, ALU.is_equal, None, ["cR"])
    mkcol("m15m", col("m15"), -1.0, None, ALU.add, None, ["cm15"])
    for t in range(RO - 1):
        mkcol("r%d" % t, col("R"), float(13 + t), None, ALU.is_equal, None, ["cR"])
        mkcol("nr%d" % t, col("R"), float(13 + t), None, ALU.not_equal, None, ["cR"])
    mkcol("d128", col("R"), 15.0, 128.0, ALU.is_lt, ALU.mult, ["cR"])
    mkcol("x16", col("m15"), -16.0, None, ALU.mult, None, ["cm15"])
    tt(newcol("RP"), col("R"), col("x16"), ALU.add, ["cR", "cx16"], ["cRP"], 1)
    J1, JM1 = T.J[:, 0:128], T.JM[:, 0:128]
    for u, h, n_ in ((0, 0, "P"), (1, 1, "P"), (0, 1, "Pp16"), (1, 0, "Pm16")):
        nm = "SW%d%d" % (u, h)
        ts(T[nm][:], J1, col(n_), col("U%d" % u), ALU.is_equal, ALU.mult, ["J", "c" + n_, "cU%d" % u], [nm])
    ts(T.IDb[:], J1, col("P"), None, ALU.is_equal, None, ["J", "cP"], ["IDb"])
    ts(T.BOb[:], T.JG[:], col("G"), None, ALU.is_equal, None, ["JG", "cG"], ["BOb"])
    ts(T.ta[:, 0:128], JM1, float(NM), None, ALU.is_lt, None, ["JM"], ["ta0"])
    tt(T.ZS[:], T.ta[:, 0:128], T.BOb[:], ALU.mult, ["ta0", "BOb"], ["ZS"], 128, 2)
    ts(T.W1[:], T.J[:, 0:144], col("G15"), None, ALU.is_equal, None, ["J", "cG15"], ["W1"], 144)
    ts(T.W2[:], T.J[:, 0:144], col("G15"), -2.0, ALU.is_equal, ALU.mult, ["J", "cG15"], ["W2"], 144)
    ts(T.tb[:, 0:128], JM1, 15.0, -16.0, ALU.is_equal, ALU.mult, ["JM"], ["tb0"])
    tt(T.JP[:], T.tb[:, 0:128], JM1, ALU.add, ["tb0", "JM"], ["JP"], 128, 2)
    ts(T.ta[:, 128:256], T.JP[:], col("RP"), -2.0, ALU.is_lt, ALU.mult, ["JP", "cRP"], ["ta1"])
    ts(T.tb[:, 128:256], T.JP[:], col("RP"), None, ALU.is_equal, None, ["JP", "cRP"], ["tb1"])
    tt(T.tc[:, 0:128], T.ta[:, 128:256], T.tb[:, 128:256], ALU.add, ["ta1", "tb1"], ["tc0"], 128, 2)
    tt(T.tc[:, 128:256], T.tc[:, 0:128], T.BOb[:], ALU.mult, ["tc0", "BOb"], ["tc1"], 128, 2)
    for t in range(RO):
        nm = "rv%d" % t
        mkcol(nm, col("RP"), float(13 + t), None, ALU.is_lt, None, ["cRP"])
        ts(T.td[:, 0:128], T.JP[:], float(13 + t), col(nm), ALU.is_lt, ALU.mult, ["JP", "c" + nm], ["td0"])
        tt(T["TRI%d" % t][:], T.td[:, 0:128], T.tc[:, 128:256], ALU.mult, ["td0", "tc1"], ["TRI%d" % t], 128, 2)
    ts(T.BOh[:], T.JG[:], col("G"), None, ALU.is_equal, None, ["JG", "cG"], ["BOh"])
    ts(T.IDh[:], J1, col("P"), None, ALU.is_equal, None, ["J", "cP"], ["IDh"])
    ts(T.ta[:], T.JM[:], col("R"), 8192.0 + CEN + 1, ALU.is_equal, ALU.mult, ["JM", "cR"], ["ta0", "ta1"], 256)
    ts(T.MKl[:], T.ta[:], -8192.0, None, ALU.add, None, ["ta0", "ta1"], ["MKl"], 256)
    ts(T.RS[:], T.JM[:], 0.0, None, ALU.is_gt, None, ["JM"], ["RS"], 256)
    ts(T.tb[:, 0:128], JM1, col("R"), col("d128"), ALU.is_ge, ALU.mult, ["JM", "cR", "cd128"], ["tb0"])
    ts(T.tb[:, 128:256], JM1, 15.0, None, ALU.is_lt, None, ["JM"], ["tb1"])
    tt(T.tc[:, 0:128], T.tb[:, 0:128], T.tb[:, 128:256], ALU.mult, ["tb0", "tb1"], ["tc0"], 128, 2)
    tt(T.DEAD[:], T.tc[:, 0:128], T.BOb[:], ALU.mult, ["tc0", "BOb"], ["DEAD"], 128, 2)
    stage[0] = 5
    ts(T.tb[:, 128:256], JM1, col("R"), 8192.0, ALU.is_equal, ALU.mult, ["JM", "cR"], ["tb1"])
    ts(T.MK0[:], T.tb[:, 128:256], -8192.0, None, ALU.add, None, ["tb1"], ["MK0"])
    ts(T.MK2[:], T.JM[:], col("R"), float(B - 1), ALU.is_equal, ALU.mult, ["JM", "cR"], ["MK2"], 256)
    ts(T.NBb[:], T.JG[:], col("G"), -float(2 ** 23), ALU.is_equal, ALU.mult, ["JG", "cG"], ["NBb"])
    ts(T.FBb[:], T.JG[:], col("G"), 2.0 ** -10, ALU.is_equal, ALU.mult, ["JG", "cG"], ["FBb"])
    ts(T.ta[:, 0:128], JM1, col("R"), -float(2 ** 23), ALU.is_gt, ALU.mult, ["JM", "cR"], ["ta0"])
    ts(T.ta[:, 128:256], JM1, col("R"), 2.0 ** -10, ALU.is_le, ALU.mult, ["JM", "cR"], ["ta1"])
    tt(T.td[:, 128:256], T.ta[:, 0:128], T.ta[:, 128:256], ALU.add, ["ta0", "ta1"], ["td1"], 128, 2)
    tt(T.MTb[:], T.td[:, 128:256], T.BOb[:], ALU.mult, ["td1", "BOb"], ["MTb"], 128, 2)
    for d, n1, n2 in (("1", "Pp16", "Pm112"), ("2", "Pp32", "Pm96"), ("3", "Pp48", "Pm80")):
        ts(T.ta[:, 0:128], J1, col(n1), None, ALU.is_equal, None, ["J", "c" + n1], ["ta0"])
        ts(T.tb[:, 0:128], J1, col(n2), None, ALU.is_equal, None, ["J", "c" + n2], ["tb0"])
        tt(T["PM" + d][:], T.ta[:, 0:128], T.tb[:, 0:128], ALU.add, ["ta0", "tb0"], ["PM" + d], 128, 2)
    for t in range(RO - 1):
        ts(T["NW%d" % t][:], T.J[:], float(W0N + K * t), col("r%d" % t), ALU.add, ALU.mult, ["J", "cr%d" % t], ["NW%d" % t], 256)
    ts(T.tb[:, 128:144], T.J[:, 0:16], 16.0, None, ALU.mult, None, ["J"], ["tb1"], 16)
    ts(T.TR[:], T.tb[:, 128:144], col("R"), None, ALU.add, None, ["tb1", "cR"], ["TR"], 16)

    def un(name, u):
        return T[name][:, W * u:W * u + W]

    def tab(name, u):
        return T[name][:, WB * u:WB * u + WB]

    def last16(name, u):
        return T[name][:, W * u + 15:W * u + W:16]

    def pz(u, n):
        return T["pc%d" % u][:, 0:n]

    def pe(u):
        return T["pc%d" % u][:, 256:256 + W]

    def pc(u):
        return T["pc%d" % u][:, 384:384 + W]

    def xw(t):
        return T.X[:, 0:B + W0N + K * t]

    def aw(t):
        return T.A[:, 0:B + W0N + K * t]

    def prep(t, u):
        s = str(u)
        ts(un("AT", u), aw(t).indirect(tab("NL", u)), float(-CEN), None, ALU.add, None, AK + ["NL" + s], ["AT" + s], W, 1, GAT)
        nb = W // 32
        o = W * u
        for b in range(nb):
            op("V", lambda b=b: g.vector.transpose(T.T1[:, o + b:o + W:nb] if nb > 1 else T.T1[:, o:o + W],
                                                   T.AT[:, o + 32 * b:o + 32 * b + 32]), ["AT" + s], ["T1%s%d" % (s, b)], vd(32))
        lst = []
        for v in range(2):
            for h in range(2):
                lst.append((T["pc" + s][:, 384 + v:384 + W:2], T["SW%d%d" % (v, h)][:],
                            T.T1[:, o + W // 2 * h:o + W // 2 * h + W // 2], h == 0, h == 1))
        mms(lst, ["T1%s%d" % (s, b) for b in range(nb)] + ["SW00", "SW01", "SW10", "SW11"], ["pc" + s], W // 2)
        n = WB * (13 + t)
        ts(T.LT[:, o:o + n], T["pc" + s][:, 384:384 + n], float(CEN + B), None, ALU.add, None, ["pc" + s], ["LT" + s], n)

    def bulk(t, u, step):
        s = str(u)
        nl = 13 + t
        o = 15 * W * u
        pd = T["pd" + s][:, 0:W]
        mms([(T["pc" + s][:, W * j:W * j + W], T.IDb[:], un("z", u), True, True) for j in range(MC)], ["IDb", "z" + s], ["pc" + s], W)
        mms([(pd, T.ZS[:], un("z", u), True, False)], ["ZS", "z" + s], ["pd" + s], W)
        for k in range(step):
            mms([(pd, T.DEAD[:], un("sel%d" % k, u), False, False)], ["DEAD", "sel%d%s" % (k, s)], ["pd" + s], W)
        n2 = min(NM, nl)
        for a in range(0, n2, GC):
            b = min(a + GC, n2)
            x = "xg%s%d" % (s, a)
            act(T.xg[:, o + W * a:o + W * b], xw(t).indirect(T.LT[:, W * u + WB * a:W * u + WB * b]), ACT.Identity, 160.0, 1.0,
                XK + ["LT" + s], [x], W * (b - a), GAT)
            for c in range(a, b, MC):
                d = min(c + MC, b)
                h = slice(o + W * c, o + W * d)
                m = "mn%s%d" % (s, c)
                tt(T.mn[:, h], T.xg[:, h], pz(u, W * (d - c)), ALU.min, [x, "pc" + s], [m], W * (d - c))
                mms([(pd, T.W1[:, 15 - i:143 - i], T.xg[:, o + W * i:o + W * i + W], False, False) for i in range(c, d)],
                    ["W1", x], ["pd" + s], W)
                mms([(pd, T.W2[:, 15 - i:143 - i], T.mn[:, o + W * i:o + W * i + W], False, i == nl - 1) for i in range(c, d)],
                    ["W2", m], ["pd" + s], W)
        for i in range(n2, nl):
            h = slice(o + W * i, o + W * i + W)
            x, m = "xg%s%d" % (s, i), "mn%s%d" % (s, i)
            tt(T.xg[:, h], xw(t).indirect(T.LT[:, W * u + WB * i:W * u + WB * i + WB]), un("z", u), ALU.subtract,
               XK + ["LT" + s, "z" + s], [x], W, 1, GAT)
            act(T.mn[:, h], T.xg[:, h], ACT.Abs, 160.0, 1.0, [x], [m], W)
            mms([(pd, T.W1[:, 15 - i:143 - i], T.mn[:, h], False, i == nl - 1)], ["W1", m], ["pd" + s], W)

    def choose(t, u, step):
        s = str(u)
        k = "sel%d" % step
        ts(un("ok", u), T["pd" + s][:, 0:W], 68.0, None, ALU.is_lt, None, ["pd" + s], ["ok" + s], W)
        mms([(pe(u), T["TRI%d" % t][:], un("ok", u), True, True)], ["TRI%d" % t, "ok" + s], ["pc" + s], W)
        ts(un(k, u), pe(u), 0.0, None, ALU.max, None, ["pc" + s], [k + s], W)
        mms([(pc(u), T.IDh[:], T.MKl[:, 0:W], True, False)], ["IDh", "MKl"], ["pc" + s], W)
        tt(un("sA", u), un(k, u), un("AT", u), ALU.mult, [k + s, "AT" + s], ["sA" + s], W, 2)
        mms([(pc(u), T.BOh[:], un("sA", u), False, True)], ["BOh", "sA" + s], ["pc" + s], W)
        scn(un("sc", u), pc(u), W, ["pc" + s], ["sc" + s])
        ts(tab("NL", u), last16("sc", u), float(B - 1), None, ALU.add, None, ["sc" + s], ["NL" + s], WB)

    def advance(t, u):
        s = str(u)
        tt(un("s", u), xw(t).indirect(tab("NL", u)), un("z", u), ALU.add, XK + ["NL" + s, "z" + s], ["s" + s], W, 1, GAT)
        act(un("z", u), un("s", u), ACT.Identity, 79.75, 0.5, ["s" + s], ["z" + s], W)

    peers = [T.cores[q] for q in range(len(T.cores)) if q != rank]

    def finish(t, u):
        s = str(u)
        act(un("yg", u), xw(t).indirect(tab("NL", u)), ACT.Identity, 160.0, 1.0, XK + ["NL" + s], ["yg" + s], W, GAT)
        mms([(pe(u), T.BOh[:], un("sA", u), True, True)], ["BOh", "sA" + s], ["pc" + s], W)
        cp(un("vb", u), pe(u), ["pc" + s], ["vb" + s], W)
        ts(tab("vT", u), last16("sc", u), float(-CEN - 1), None, ALU.add, None, ["sc" + s], ["vT" + s], WB)
        ts(tab("vX", u), last16("sc", u), float(B + CEN), None, ALU.add, None, ["sc" + s], ["vX" + s], WB)
        tt(un("gt", u), un("yg", u), un("z", u), ALU.is_gt, ["yg" + s, "z" + s], ["gt" + s], W, 2)
        mms([(pc(u), T.IDh[:], T.MK0[:, 0:W], True, False)], ["IDh", "MK0"], ["pc" + s], W)
        mms([(pc(u), T.BOb[:], un("gt", u), False, True)], ["BOb", "gt" + s], ["pc" + s], W)
        scn(un("sv", u), pc(u), W, ["pc" + s], ["sv" + s])
        ts(tab("wt", u), last16("sv", u), 9.0, 2.0 ** -9, ALU.is_lt, ALU.add, ["sv" + s], ["wt" + s], WB)
        tt(un("s2", u), un("yg", u), un("z", u), ALU.add, ["yg" + s, "z" + s], ["s2" + s], W, 2)
        act(un("z", u), un("s2", u), ACT.Identity, -0.25, 0.5, ["s2" + s], ["z" + s], W)
        for b in range(W // 64):
            q = W // 64 * u + b
            d = (q - rank) % len(T.cores)
            zz = T.z[:, 64 * q:64 * q + 64]
            if d == 0:
                c0 = B + W0N + K * t + 64 * rank
                act(T.X[:, c0:c0 + 64], zz, ACT.Identity, -160.0, 1.0, ["z" + s], ["Xo%d" % t], 64)
            else:
                k = q if q < rank else q - 1
                pp = T["pc" + s][:, 64 * b:64 * b + 64]
                mms([(pp, T["PM%d" % d][:], zz, True, True)], ["PM%d" % d, "z" + s], ["pc" + s], 64)
                act(T.snd[:, 64 * k:64 * k + 64], pp, ACT.Identity, -160.0, 1.0, ["pc" + s], ["snd%d" % k], 64)

    def send(t):
        used = []
        trs = [None] * len(peers)
        c0 = B + W0N + K * t + 64 * rank
        for k in sorted(range(len(peers)), key=lambda k: topo.chip(peers[k]) == topo.chip(core)):
            en = [e for e in topo.engines(core, peers[k]) if e not in used][:4]
            used += en
            rid, pid = topo.addr(peers[k])[:2]
            trs[k] = RemoteDMATransfer(dst_ids=[DstId(rid=rid, pnc=pid)], dma_engine_mask=sum(1 << e for e in en),
                                       remote_sem=T.sem["arr%d" % t], src=T.snd[:, 64 * k:64 * k + 64], dst=T.X[:, c0:c0 + 64])
        rec("G", "send", lambda: g.remote_dma_fused(trs, local_sem=T.sem.snt), ["snd%d" % k for k in range(len(peers))],
            ["Xa%d" % t], 1.5, 4.0, "arr%d" % t)

    def pairs(k, c0, c1):
        u = k // WB
        ts(T.EQ[:, 256 * k + c0:256 * k + c1], T.vb[:, c0:c1], T.vT[:, k:k + 1], T.wt[:, k:k + 1], ALU.is_equal, ALU.mult,
           ["vb%d" % v for v in range(c0 // W, c1 // W)] + ["vT%d" % u, "wt%d" % u], ["EQ%d_%d" % (k, c0)], c1 - c0, 0.5)

    def sums(ps, k, c0, c1, mats, last=False):
        a, b = 16 * k, 16 * k + 16
        lst = []
        nn = 0
        for lo, hi, m in ((c0, min(a, c1), "FBb"), (a, b, "MTb"), (max(b, c0), c1, "NBb")):
            if lo < hi and lo >= c0 and hi <= c1 and m in mats:
                lst.append((T[ps][:, lo:hi], T[m][:], T.EQ[:, 256 * k + lo:256 * k + hi], False, last))
                nn += max(64, hi - lo)
        if lst:
            mms(lst, list(mats) + ["EQ%d_%d" % (k, c0)], [ps], nn / len(lst))

    def joint(u):
        s = str(u)
        if u == 0:
            mms([(T.pd0[:, 0:256], T.IDh[:], T.MKl[:], True, False), (T.pd0[:, 0:256], T.IDh[:], T.MK2[:], False, False)],
                ["IDh", "MKl", "MK2"], ["pd0"], 256)
        mms([(T.pd0[:, W * u:W * u + W], T.BOh[:], un("sA", u), False, False)], ["BOh", "sA" + s], ["pd0"], W)
        for k in range(WB * u):
            pairs(k, W * u, W * u + W)
            sums("pd0", k, W * u, W * u + W, ("NBb",))
        for k in range(WB * u, WB * u + WB):
            pairs(k, 0, W * u + W)
            if u < NU - 1:
                sums("pd0", k, 0, W * u + W, ("FBb", "MTb", "NBb"))
            else:
                sums("pd0", k, 0, K, ("MTb", "NBb"), k == 15)

    def settle(t):
        f = T.scL[:, 15:256:16]
        scn(T.scL[:], T.pd0[:, 0:256], 256, ["pd0"], ["scL"])
        if t < RO - 1:
            tt(T.ofs[:], f, T.TR[:], ALU.max, ["scL", "TR"], ["ofs"], 16, 2)
            cp(T.OFF[:], T.ofs[:], ["ofs"], ["OFF"], 16)
            cp(aw(t).indirect(T.OFF[:]), T.VA[:], ["VA", "OFF"], AK, 256, 3.0)
        stage[0] = 20 * t + 17.5
        mms([(T.pd1[:, 0:256], T.IDh[:], T.MKl[:], True, False)], ["IDh", "MKl"], ["pd1"], 256)
        for k in range(16 - WB, 16):
            sums("pd1", k, 0, 256, ("FBb",), k == 15)
        tt(T.fd[:], f, T.vX[:], ALU.subtract, ["scL"] + ["vX%d" % u for u in range(NU)], ["fd"], 16, 2)
        scn(T.scM[:], T.pd1[:, 0:256], 256, ["pd1"], ["scM"])
        tt(T.fe[:], T.fd[:], T.scM[:, 15:256:16], ALU.add, ["fd", "scM"], ["fe"], 16, 2)
        ts(T.ff[:], T.fe[:], 0.0007, None, ALU.is_lt, None, ["fe"], ["ff"], 16)
        tt(T.fm[:], T.ff[:], f, ALU.mult, ["ff", "scL"], ["fm"], 16, 2)
        tt(T.fo[:], T.fm[:], T.TR[:], ALU.max, ["fm", "TR"], ["fo"], 16, 2)
        cp(T.OFX[:], T.fo[:], ["fo"], ["OFX"], 16)
        cp(xw(t).indirect(T.OFX[:]), T.VX[:], ["VX", "OFX"], XK, 256, 3.0)

    def newlinks(t):
        ts(T.AF[:], aw(t).indirect(T.NL[:]), col("nr%d" % t), None, ALU.mult, None,
           AK + ["NL%d" % u for u in range(NU)] + ["cnr%d" % t], ["AF"], 256, 1, GAT)
        tt(T.VA[:], T.AF[:], T["NW%d" % t][:], ALU.add, ["AF", "NW%d" % t], ["VA"], 256, 2)
        c0 = B + W0N + K * t
        ts(T.A[:, c0:c0 + K], T.AF[:], col("m15"), col("m15m"), ALU.mult, ALU.add, ["AF", "cm15", "cm15m"], ["An%d" % t], 256)

    for t in range(RO):
        for u in range(NU):
            stage[0] = 20 * t + 1 + u
            s = str(u)
            act(un("z", u), xw(max(t - 1, 0)).indirect(tab("NL", u)), ACT.Identity, 160.0, 1.0, XK + ["NL" + s], ["z" + s], W, GAT)
            prep(t, u)
        if t:
            XK = XK + ["Xa%d" % (t - 1), "Xo%d" % (t - 1)]
        for st in range(S):
            for u in range(NU):
                stage[0] = 20 * t + 1 + NU * st + u
                bulk(t, u, st)
                choose(t, u, st)
                if st < S - 1:
                    prep(t, u)
                    advance(t, u)
                else:
                    finish(t, u)
                    stage[0] = 20 * t + 16.5
                    joint(u)
        stage[0] = 20 * t + 17
        send(t)
        act(T.VX[:], T.yg[:], ACT.Identity, col("fb"), col("fs"), ["yg%d" % u for u in range(NU)] + ["cfb", "cfs"], ["VX"], 256)
        if t < RO - 1:
            newlinks(t)
        else:
            ts(T.vout[:], T.vb[:], float(CEN), None, ALU.add, None, ["vb%d" % u for u in range(NU)], ["vout"], 256)
            dma("Y", T.yv[:], T.vout[0:128:16, :], "dO", ["vout"], [], 2.0)
        settle(t)
        if t < RO - 1:
            AK = AK + ["An%d" % t]
    XK = XK + ["Xa%d" % (RO - 1), "Xo%d" % (RO - 1)]
    dma("Y", T.yx[:], T.X[:, B:B + W0N + RO * K], "dO", XK, [], 5.0)

    n = len(recs)
    preds = [set() for _ in range(n)]
    lw, lr = {}, {}

    def bank(k):
        return k[0] == "p"

    for i, r in enumerate(recs):
        reads, writes = r[3], r[4]
        for k in reads:
            if k in lw:
                preds[i].add(lw[k])
            lr.setdefault(k, []).append(i)
        for k in writes:
            if k in lw:
                preds[i].add(lw[k])
            preds[i].update(lr.get(k, []))
        for k in reads + writes:
            if bank(k) or k in writes:
                lw[k] = i
                lr[k] = []
        preds[i].discard(i)
    succ = [[] for _ in range(n)]
    for i in range(n):
        for j in preds[i]:
            succ[j].append(i)
    prio = [0.0] * n
    for i in range(n - 1, -1, -1):
        prio[i] = recs[i][5] + recs[i][6] + max([prio[j] + WK for j in succ[i]], default=0.0)
    left = [len(p) for p in preds]
    ready = [0.0] * n
    avail = {q: [] for q in QUE}
    for i in range(n):
        if left[i] == 0:
            avail[recs[i][0]].append(i)
    tq = {q: 0.0 for q in QUE}
    order = []
    while len(order) < n:
        best = None
        for q in QUE:
            if avail[q]:
                e = min(max(tq[q], ready[i]) for i in avail[q])
                if best is None or e < best[0]:
                    best = (e, q)
        e, q = best
        c = [i for i in avail[q] if max(tq[q], ready[i]) <= e + LOOK]
        i = max(c, key=lambda j: (-recs[j][8], prio[j], -j))
        avail[q].remove(i)
        tq[q] = max(tq[q], ready[i]) + recs[i][5]
        end = tq[q] + recs[i][6]
        order.append(i)
        for j in succ[i]:
            same = recs[j][0] == q == "P"
            ready[j] = max(ready[j], tq[q] if same else end + WK)
            left[j] -= 1
            if left[j] == 0:
                avail[recs[j][0]].append(j)

    cnt = {}
    known = {q: {} for q in QUE}
    lastw, lastr = {}, {}

    def need(q, tok):
        sem, val, clk = tok
        kn = known[q]
        if kn.get(sem, 0) >= val:
            return
        QUE[q].wait_ge(T.sem[sem], val)
        kn[sem] = val
        for s_, v_ in clk.items():
            if kn.get(s_, 0) < v_:
                kn[s_] = v_

    total = {}
    for r in recs:
        if r[1] == "dma":
            total[r[7]] = total.get(r[7], 0) + 16
    for i in order:
        q, kind, fn, reads, writes, dur, lat, sem, stg = recs[i]
        toks = []
        for k in reads:
            if bank(k):
                toks += [x for q2, x in lastr.get(k, {}).items() if q2 != q]
            elif k in lastw:
                toks.append(lastw[k])
        for k in writes:
            if k in lastw:
                toks.append(lastw[k])
            toks += [x for q2, x in lastr.get(k, {}).items() if q2 != q or not bank(k)]
        for x in sorted(toks, key=lambda x: -x[1]):
            need(q, x)
        if kind == "op":
            sm = "q" + q
            cnt[sm] = cnt.get(sm, 0) + 1
            fn().then_inc(T.sem[sm], 1)
            tok = rtok = (sm, cnt[sm], dict(known[q]))
            who = q
        elif kind == "dma":
            fn().then_inc(T.sem[sem], 16)
            cnt[sem] = total[sem]
            tok = rtok = (sem, total[sem], dict(known[q]) if total[sem] == 16 else {})
            who = q + sem
        else:
            fn()
            cnt["snt"] = cnt.get("snt", 0) + 4 * len(peers)
            rtok = ("snt", cnt["snt"], dict(known[q]))
            cnt[sem] = 4 * len(peers)
            tok = (sem, cnt[sem], {})
            who = "rem"
        for k in writes:
            if bank(k):
                lastr.setdefault(k, {})[q] = tok
            else:
                lastw[k] = tok
                lastr[k] = {}
        for k in reads:
            lastr.setdefault(k, {})[who] = rtok
    for sem, val in cnt.items():
        need("Y", (sem, val, {}))
